import numpy as np, ml_dtypes
CORES = [3,7,11,15,131,135,139,143]
N = 8
import mx_ref
BF = ml_dtypes.bfloat16
def gentries(a):
    return np.ascontiguousarray(a.reshape(8, 16, -1).transpose(0, 2, 1)).reshape(8, -1)
def gtable(e):
    e = np.asarray(e); return np.ascontiguousarray(e.reshape(8, -1, 16).transpose(0, 2, 1)).reshape(128, -1).astype(np.int32)
def gcols(t, e):
    v = np.concatenate([t.reshape(8, 16, -1, 4), np.zeros((8, 16, 1, 4), BF)], axis=2)
    return np.ascontiguousarray(np.stack([v[g][:, e[g]] for g in range(8)])).reshape(128, -1)
def gpick(z, e):
    return np.concatenate([z[16 * g:16 * g + 16][:, e[g]] for g in range(8)])
def tile(rs):
    return np.stack(rs, axis=2).reshape(128, -1).astype(BF)
def pick(q, e):
    c = np.concatenate([q[0].reshape(128, -1, 4), np.zeros((128, 1, 4), np.uint8)], axis=1); s = np.concatenate([q[1], np.ones((16, 1), np.uint8)], axis=1)
    return (np.ascontiguousarray(c[:, e].reshape(128, -1)), np.ascontiguousarray(s[:, e]))
def join(*qs):
    return (np.concatenate([q[0] for q in qs], axis=1), np.concatenate([q[1] for q in qs], axis=1))
def put(q, e, v):
    c, s = q[0].reshape(128, -1, 4).copy(), q[1].copy(); c[:, e] = v[0].reshape(128, -1, 4); s[:, e] = v[1]
    return (c.reshape(128, -1), s)
def pk(c, s):
    return (np.ascontiguousarray(c), mx_ref.live(s))
def emit(q):
    return q[0], q[1]
def packed(v, rng):
    q = [mx_ref.quantize(np.ascontiguousarray(v[r])) for r in range(N)]
    return np.stack([a for a, b in q]), np.stack([mx_ref.plane(b, rng) for a, b in q])
def values_of_codes():
    e, c = np.zeros((128, 128, 4), np.float32), np.zeros((128, 2, 4), np.uint8)
    e[np.arange(128), np.arange(128), 0] = 1
    c[:127, :, 0] = np.arange(256).reshape(2, 128).T[:127]
    return mx_ref.matmul(mx_ref.quantize(e.reshape(128, 512).astype(BF)), (c.reshape(128, 8), np.full((16, 2), 127, np.uint8))).T.reshape(-1).astype(np.float64)
CODE_VALUE, SCALE_VALUE = values_of_codes(), 2.0 ** (np.arange(256) - 127.0)
def decode(q):
    return (CODE_VALUE[q[0]].reshape(16, 8, -1, 4) * SCALE_VALUE[q[1]][:, None, :, None] + 0.0).reshape(128, -1).astype(np.float32)
def f(rng, *shape):
    return mx_ref.flush((rng.standard_normal(shape, dtype=np.float32) * np.exp2(rng.integers(-2, 3, shape[:-1] + (1,)))).astype(BF))
def wide(rng, *shape, cols=0):
    v = rng.standard_normal(shape, dtype=np.float32) * np.exp2(rng.integers(-12, 13, shape)).astype(np.float32)
    if cols: v *= np.repeat(np.exp2(rng.integers(-cols, cols + 1, shape[:-2] + (1, shape[-1] // 4))) * (rng.random(shape[:-2] + (1, shape[-1] // 4)) > 0.0625), 4, axis=-1).astype(np.float32)
    return mx_ref.flush(v.astype(BF))
C = 320
MASK = [1, 2, 4]
PARITY = np.array([(r ^ (r >> 1) ^ (r >> 2)) & 1 for r in range(N)])
def numbers_of(rng):
    return {"x": np.array(f(rng, N, 128, 4 * C)), "u": np.array(f(rng, N, 128, 512)), "v": np.array(f(rng, N, 128, 512))}
def stored(k):
    return {"fl": np.stack([gtable(k[r]) for r in range(N)])}
def lists(rng):
    return stored(rng.permuted(np.tile(np.arange(C), (N, 8, 1)), axis=2))
def layers(rng):
    return np.array(f(rng, N, 128, 2048)).reshape(N, 8, 16, 4, 8, 16, 4)
def weights(rng, w):
    c, p = packed(np.ascontiguousarray(w).reshape(N, 128, 2048), rng)
    return {"wc": c, "ws": p}
def setup_inputs(rng):
    return {**numbers_of(rng), **lists(rng), **weights(rng, layers(rng))}
def setup_inputs_long(rng):
    d = numbers_of(rng)
    kind = rng.permutation(8)
    s = np.tile(rng.choice([-1.0, 1.0], (8, C)), (N, 1, 1))
    k = np.zeros((N, 8, C), np.int64)
    for g in range(8):
        c, p = rng.permutation(C), int(rng.integers(C))
        if kind[g] == 0: c, p = np.arange(C), C - N // 2
        if kind[g] == 1: c = np.arange(C)[::-1]
        k[:, g, c] = np.roll(c, -1)
        for r in range(N):
            if kind[g] in (0, 1, 3, 4): s[r, g, c[(p + r) % C]] *= -1
            if kind[g] == 2 and PARITY[r]: s[r, g, c[p]] *= -1
            if kind[g] == 6 and PARITY[r]: s[r, g] *= -1
            if kind[g] == 7:
                s[r, g] = rng.choice([-1.0, 1.0], C)
                k[r, g] = np.arange(C)
    x = d["x"].reshape(N, 8, 16, C, 4)
    x[:, :, 0] = 0
    x[:, :, 0, :, 0] = s.astype(np.float32).astype(BF)
    u = d["u"].reshape(N, 128, 128, 4)
    u[:, :, ::16] = 0
    for h in range(0, 128, 16): u[:, h, h, 0] = 1
    w = layers(rng)
    w[:, :, :, :, :, 0] = 0
    return {"x": x.reshape(N, 128, 4 * C), "u": u.reshape(N, 128, 512), "v": d["v"], **stored(k), **weights(rng, w)}
def setup_inputs_near(rng):
    d = numbers_of(rng)
    o, e = rng.permutation(N) % 2, rng.permutation(N)
    k = np.where(o == 0, 2.0 ** -27, 1.0)
    m = np.where(o == 0, 2.0 ** -30, 1.0)
    s = rng.integers(-1, 2, (N, 8, C))
    s[e[0]] = 0
    s[e[1]] = 1
    x = d["x"].astype(np.float32).reshape(N, 8, 16, C, 4)
    x[o == 0] = 0
    x[:, :, :3] = 0
    x[:, :, 8:] = 0
    x[:, :, 0, :, 0] = np.where(s == 0, 1.0, 1.125 * s) * k[:, None, None]
    x[:, :, 1, :, 0] = np.where(s == 0, -1.125, -1.25 * s) * k[:, None, None]
    x[:, :, 3, :, 0] = k[:, None, None]
    x[:, :, 8, :, 0] = rng.choice([-1.0, 1.0], (N, 8, C)) * 2.0 ** -30
    x[:, :, 9, :, 0] = 2.0 ** -26
    for r in range(N):
        for g in rng.permutation(8)[:4]: x[r, g, 0, rng.integers(C), 0] = 2.0 ** 30 * rng.choice([-1.0, 1.0])
    u = d["u"].reshape(N, 128, 128, 4)
    u[:, :, ::16] = 0
    for h in range(0, 128, 16):
        u[:, h, h, 0] = (1.125 * m).astype(np.float32).astype(BF)
        u[:, h + 1, h, 0] = m.astype(np.float32).astype(BF)
        u[:, h + 2, h, 0] = m.astype(np.float32).astype(BF)
    w = layers(rng)
    w[:, :, :, :, :, :10] = 0
    for g in range(8): w[:, g, 8, 0, g, 2, 0] = 2.0 ** -7
    return {"x": x.reshape(N, 128, 4 * C).astype(BF), "u": u.reshape(N, 128, 512), "v": d["v"], **lists(rng), **weights(rng, w)}
def setup_inputs_odd(rng):
    d = numbers_of(rng)
    e = (PARITY[:, None] + rng.permutation(8)) % 2
    a = 1.0 + (2 * rng.integers(0, 64, (N, 8, 16, C, 4)) + 1) * 2.0 ** -7
    x = np.zeros((N, 8, 16, C, 4))
    x[:, :, :8] = a[:, :, :8] * np.exp2(-rng.integers(0, 7, (N, 8, 8, C, 4)).astype(np.float64)) * rng.choice([-1.0, 1.0], (N, 8, 8, C, 4))
    x[:, :, 0] = 0
    x[:, :, 0, :, 0] = 1.96875 * 2.0 ** 8 * rng.choice([-1.0, 1.0], (N, 8, C))
    x[:, :, 8:] = np.where(e[:, :, None, None, None] == 0, a[:, :, 8:] * np.exp2(12.0 - rng.integers(8, 15, (N, 8, 8, C, 4))), 0.0)
    x[:, :, 8, :, 0] = (np.where(e == 0, -1.0, 1.0) * 1.96875 * 2.0 ** 12)[:, :, None]
    u = d["u"].reshape(N, 128, 128, 4)
    u[:, 8::16, ::16] = 0
    w = layers(rng)
    for i in (0, 8):
        w[:, :, i] = 0
        w[:, :, :, :, :, i] = 0
    for g in rng.permutation(8)[:4]:
        x[:, g, :3] = 0
        x[:, g, 0, :, 0] = 1.96875 * 2.0 ** 8
        x[:, g, 1, :, 0] = (8 + rng.integers(-1, 2, (N, C))) * 2.0 ** -8
        x[:, g, 2, :, 0] = -2.0 ** -5
        x[:, g, 8:] = 0
        x[:, g, 8, :, 0] = 1.96875 * 2.0 ** 12
        x[:, g, 9] = rng.integers(1, 16, (N, C, 4)) * 2.0 ** -4
        u[:, 16 * g, ::16] = 0
        u[:, :, 16 * g] = 0
        u[:, 16 * g + 1:16 * g + 3, 16 * g, 0] = 1
        w[:, :, :, :, g] = 0
        for i in (0, 8): w[:, g, i, 0, g, i, 0] = -0.5
        for b in range(4): w[:, g, 9, b, g, 10, b] = 256.0
    return {"x": x.astype(np.float32).reshape(N, 128, 4 * C).astype(BF), "u": u.reshape(N, 128, 512), "v": d["v"], **lists(rng), **weights(rng, w)}
def setup_inputs_ends(rng):
    d = numbers_of(rng)
    x = np.zeros((N, 8, 16, C, 4))
    u = d["u"].astype(np.float32).reshape(N, 128, 128, 4)
    v = np.zeros((N, 128, 512))
    w = np.zeros((N, 128, 4, 128, 4), np.float32)
    o = rng.permutation(N) % 4
    third, others = np.flatnonzero(o == 2), np.flatnonzero(o != 2)
    if len(third) == 2 and third[0] ^ third[1] == MASK[0]:
        p = rng.choice(others)
        o[third[1]] = o[p]
        o[p] = 2
    i, at = np.arange(128), np.arange(C)
    k = np.zeros((N, 8, C), np.int64)
    for r in range(N):
        h = rng.permutation(8)
        c = np.where(h < 2, 0.0, h % 2 * 2.0 - 1.0)[None, :, None]
        low = -(0.9 + 0.1 * rng.random((8, 16, C, 4))) * 2.0 ** 30
        if o[r] == 0: x[r] = low
        if o[r] == 1: x[r] = low * rng.choice([-1.0, 1.0], C)[:, None]
        if o[r] == 2: x[r] = -(1.0 + 0.125 * rng.integers(0, 8, (8, 16, C, 4))) * 2.0 ** -30
        if o[r] == 3: x[r] = d["x"][r].astype(np.float32).reshape(8, 16, C, 4)[:, :, :1]
        if o[r] < 2:
            u[r, :, ::16] = c * (0.9 + 0.1 * rng.random((128, 8, 4))) * 2.0 ** 30
            v[r] = rng.choice([-1.0, 1.0], (128, 512)) * (0.9 + 0.1 * rng.random((128, 512))) * 2.0 ** 30
        else: v[r] = rng.choice([-1.0, 1.0], (128, 512)) * (1.0 + 0.125 * rng.integers(0, 8, (128, 512))) * 2.0 ** -30
        if o[r] == 2: u[r, :, ::16] = c * (1.0 + 0.125 * rng.integers(0, 8, (128, 8, 4))) * 2.0 ** -30
        if o[r] == 3: u[r, :, ::16] *= np.abs(c).astype(np.float32)
        t = np.array([4.0, 8.0, 16.0])[rng.permutation(8) % 3]
        if o[r] == 2: t[:] = 2.0 ** -8
        if o[r] == 3: t[:] = 2.0 ** 5
        for b in range(4): w[r, i, b, i, b] = t[i // 16]
        for g, n in enumerate(rng.permutation(8) % 5): k[r, g] = [at, at[::-1], np.roll(at, -1), at ^ 1, rng.permutation(C)][n]
    return {"x": x.astype(np.float32).reshape(N, 128, 4 * C).astype(BF), "u": u.reshape(N, 128, 512).astype(BF), "v": v.astype(np.float32).astype(BF), **stored(k), **weights(rng, w.astype(BF))}
def setup_inputs_spread(rng):
    d = numbers_of(rng)
    w = layers(rng).reshape(N, 128, 4, 128, 4)
    i, r = np.arange(128), int(rng.integers(N))
    for b in range(4): w[r, i, b, i, b] = 256.0
    return {"x": wide(rng, N, 128, 4 * C, cols=6), "u": d["u"], "v": d["v"], **lists(rng), **weights(rng, w)}
def check_inputs(d):
    b = []
    for k in ("x", "u", "v"):
        a = np.abs(d[k].astype(np.float32))
        if not (np.isfinite(a).all() and ((a == 0) | (a >= 2.0 ** -30) & (a <= 2.0 ** 30)).all()): b.append("a value of " + k)
    none, least, most = [emit(mx_ref.quantize(np.full((128, 16), k, np.float32).astype(BF)))[1][0, 0] for k in (0.0, 2.0 ** -8, 2.0 ** 8)]
    for r in range(N):
        if not (np.sort(gentries(d["fl"][r]), axis=1) == np.arange(C)).all(): b.append("fl: a group's entries are no permutation")
        if ((d["wc"][r] == 0x7F) | (d["wc"][r] == 0xFF)).any(): b.append("wc: a code that is no number")
        s = mx_ref.live(d["ws"][r])
        if ((s != none) & ((s < least) | (s > most))).any(): b.append("ws: a scale out of range")
        if (((d["wc"][r].reshape(16, 8, 512, 4) & 0x7F) != 0) & (s == none)[:, None, :, None]).any(): b.append("wc: a code other than zero under the scale of zeros")
    return b
def returns(e, gate):
    at = np.tile(np.arange(C), (8, 1))
    step = np.where(gate, at, e)
    a = e
    for i in range(C): a = np.take_along_axis(step, a, axis=1)
    return np.where(gate, a, at)
def reference(x, u, v, fl, wc, ws):
    half = np.float32(0.5)
    qu = [mx_ref.quantize(u[r]) for r in range(N)]
    lay = [pk(wc[r], ws[r]) for r in range(N)]
    own = [gentries(fl[r]).astype(np.int64) for r in range(N)]
    now = [x[r] for r in range(N)]
    for m in MASK:
        q = [mx_ref.quantize(now[r]) for r in range(N)]
        t = [decode(q[r]) for r in range(N)]
        bit = [mx_ref.matmul(qu[r], q[r])[::16] > 0 for r in range(N)]
        made, new = [], []
        for r in range(N):
            d = r ^ m
            a = returns(own[d], bit[r] != bit[d])
            n = np.take_along_axis(own[r], a, axis=1)
            z = (gcols(t[r].astype(BF), n).astype(np.float32) + gcols(t[d].astype(BF), a).astype(np.float32)) * half
            qz = mx_ref.quantize(z.astype(BF))
            back = np.argsort(n, axis=1)
            p = [mx_ref.matmul(pick(lay[r], np.arange(128 * b, 128 * b + 128)), qz) * np.float32(0.03125) for b in range(4)]
            made.append(tile([(t[r][:, b::4] + gpick(p[b], back)) * half for b in range(4)]))
            new.append(n)
        now, own = made, new
    y, ln = np.zeros((N, 128, C), np.float32), np.zeros((N, 8, C), np.float32)
    oc, osc = np.zeros((N, 128, 4 * C), np.uint8), np.zeros((N, 16, C), np.uint8)
    for r in range(N):
        q = mx_ref.quantize(now[r])
        y[r] = mx_ref.matmul(mx_ref.quantize(v[r]), q)
        ln[r] = own[r]
        oc[r], osc[r] = emit(q)
    return {"y": y, "ln": ln, "oc": oc, "osc": osc}

@@ -1,0 +1,377 @@
+from concourse.mybir import dt, AluOpType, ActivationFunctionType
+
+C = 320
+MASK = [1, 2, 4]
+STAGES = [2, 2, 2]
+LAST = 1
+NW = 1 + sum(STAGES) + len(STAGES)
+FW2W = 1056
+
+SCRATCH = {
+    "I1": ("sbuf", [128, C], "int32"), "IB": ("sbuf", [128, C], "int32"),
+    "IOS": ("sbuf", [128, C], "bfloat16"), "MSK": ("sbuf", [128, C], "bfloat16"), "NMS": ("sbuf", [128, C], "bfloat16"),
+    "PI": ("sbuf", [128, 20], "int32"), "CI": ("sbuf", [128, 20], "int32"), "PA": ("sbuf", [128, 20], "int32"),
+    "DG": ("sbuf", [128, 128], "bfloat16"),
+    "OI": ("sbuf", [128, 8], "int32"), "UO": ("sbuf", [128, 8], "uint16"),
+    "ATS": ("sbuf", [128, 20], "float32"),
+    "ET": ("sbuf", [128, 2048], "bfloat16"),
+    "EQ": ("sbuf", [128, 512], "float8_e4m3fn_x4"), "ES": ("sbuf", [128, 512], "uint8"),
+    "UT": ("sbuf", [128, 512], "bfloat16"), "VT": ("sbuf", [128, 512], "bfloat16"),
+    "UQ": ("sbuf", [128, 128], "float8_e4m3fn_x4"), "US": ("sbuf", [128, 128], "uint8"),
+    "UQ2": ("sbuf", [128, 128], "float8_e4m3fn_x4"), "US2": ("sbuf", [128, 128], "uint8"),
+    "VQ": ("sbuf", [128, 128], "float8_e4m3fn_x4"), "VS": ("sbuf", [128, 128], "uint8"),
+    "WQ": ("sbuf", [128, 512], "float8_e4m3fn_x4"), "WS": ("sbuf", [128, 512], "uint8"),
+    "FLI": ("sbuf", [128, 20], "int32"),
+    "AI3": ("sbuf", [128, C], "bfloat16"),
+    "FW1": ("sbuf", [128, 640], "bfloat16"), "FW2": ("sbuf", [128, FW2W], "bfloat16"),
+    "MK": ("sbuf", [128, C], "bfloat16"), "SC": ("sbuf", [128, C], "bfloat16"),
+    "MK2": ("sbuf", [128, C], "bfloat16"), "SC2": ("sbuf", [128, C], "bfloat16"),
+    "LNF": ("sbuf", [128, C], "float32"), "YS": ("sbuf", [128, C], "float32"),
+    "PS": ("psum", [128, 4096], "float32"),
+}
+for _r in range(4):
+    SCRATCH.update({
+        "X%d" % _r: ("sbuf", [128, 4 * C], "bfloat16"),
+        "QX%d" % _r: ("sbuf", [128, C], "float8_e4m3fn_x4"), "SX%d" % _r: ("sbuf", [128, C], "uint8"),
+        "FS%d" % _r: ("sbuf", [128, C], "bfloat16"),
+        "FI%d" % _r: ("sbuf", [128, 20], "uint16"),
+    })
+for _r in range(3):
+    SCRATCH.update({
+        "F4%d" % _r: ("sbuf", [128, 80], "uint16"),
+        "PK%d" % _r: ("sbuf", [128, 40], "bfloat16"), "LP%d" % _r: ("sbuf", [128, 40], "bfloat16"),
+        "LQ%d" % _r: ("sbuf", [128, C], "float8_e4m3fn_x4"), "LS%d" % _r: ("sbuf", [128, C], "uint8"),
+        "XF%d" % _r: ("sbuf", [128, 4 * C], "bfloat16"),
+        "QF%d" % _r: ("sbuf", [128, C], "float8_e4m3fn_x4"), "SF%d" % _r: ("sbuf", [128, C], "uint8"),
+        "F%d" % _r: ("sbuf", [128, 3 * C], "bfloat16"), "M%d" % _r: ("sbuf", [128, 4 * C], "bfloat16"),
+        "Z%d" % _r: ("sbuf", [128, 4 * C], "bfloat16"),
+        "QZ%d" % _r: ("sbuf", [128, C], "float8_e4m3fn_x4"), "SZ%d" % _r: ("sbuf", [128, C], "uint8"),
+        "PW%d" % _r: ("sbuf", [128, 4 * C], "float32"), "B3%d" % _r: ("sbuf", [128, C], "float32"),
+        "WN%d" % _r: ("sbuf", [128, C * NW], "bfloat16"),
+        "TB%d" % _r: ("sbuf", [128, 20 * 12], "uint16"), "TF%d" % _r: ("sbuf", [128, 20 * 10], "float32"),
+        "AT%d" % _r: ("sbuf", [128, 20], "uint16"), "AI%d" % _r: ("sbuf", [128, C], "bfloat16"),
+    })
+SCRATCH["FT0"] = ("sbuf", [128, 20], "uint16")
+SEMAPHORES = ["sV", "sS", "sP", "sG", "lsent", "apl"] + ["d%d" % i for i in range(16)] + [k + str(r) for r in range(3) for k in ("apk", "aq", "asc")]
+
+
+def rank_program(g, core, T, topo):
+    rank = T.rank_of(core)
+    if rank is None:
+        return
+    A = AluOpType
+    COPY = ActivationFunctionType.Copy
+    v, s, pe = g.vector, g.scalar, g.tensor
+    queue = {"V": v, "S": s, "P": pe, "G": g, "Y": g.sync}
+
+    count = {}
+    known = {q: {} for q in queue}
+    behind = {}
+    writers, readers = {}, {}
+
+    def reg(name, lo=0, hi=None, lane=None):
+        return (name, lo, T[name].shape[1] if hi is None else hi, lane)
+
+    def meet(a, b):
+        return a[1] < b[2] and b[1] < a[2] and (a[3] is None or b[3] is None or a[3] == b[3])
+
+    def need(q, toks):
+        best = {}
+        for (sem, val) in toks:
+            if known[q].get(sem, 0) < val and best.get(sem, 0) < val:
+                best[sem] = val
+        for sem in list(best):
+            for sem2, val2 in best.items():
+                if sem2 != sem and behind.get((sem2, val2), {}).get(sem, 0) >= best[sem]:
+                    best[sem] = 0
+                    break
+        for sem, val in best.items():
+            if val:
+                queue[q].wait_ge(T.sem[sem], val)
+                known[q][sem] = max(val, known[q].get(sem, 0))
+                for k2, v2 in behind.get((sem, val), {}).items():
+                    known[q][k2] = max(v2, known[q].get(k2, 0))
+
+    def deps(q, rd, wr, dma):
+        toks = []
+        for r_ in rd:
+            toks += [t for (x, t, e) in writers.get(r_[0], []) if meet(x, r_)]
+        for w_ in wr:
+            toks += [t for (x, t, e) in writers.get(w_[0], []) if meet(x, w_) and not (q == "P" and e == q)]
+            toks += [t for (x, t, e) in readers.get(w_[0], []) if meet(x, w_) and (dma or e != q)]
+        need(q, toks)
+
+    def note(q, rd, wr, tok, e):
+        behind[tok] = dict(known[q])
+        for r_ in rd:
+            readers.setdefault(r_[0], []).append((r_, tok, e))
+        for w_ in wr:
+            writers.setdefault(w_[0], []).append((w_, tok, e))
+
+    def op(q, call, rd, wr):
+        deps(q, rd, wr, False)
+        sem = "s" + q
+        count[sem] = count.get(sem, 0) + 1
+        call().then_inc(T.sem[sem], 1)
+        note(q, rd, wr, (sem, count[sem]), q)
+
+    ndma = [0]
+
+    def dma(q, out, in_, rd, wr):
+        deps(q, rd, wr, True)
+        sem = "d%d" % ndma[0]
+        ndma[0] += 1
+        count[sem] = 16
+        queue[q].dma_start(out, in_).then_inc(T.sem[sem], 16)
+        note(q, rd, wr, (sem, 16), "dma" + sem)
+
+    def send(dst, out, in_, rd, land, sem):
+        deps("G", rd, [], True)
+        rid, pid = topo.addr(dst, core)
+        g.remote_dma(out, in_, T.sem[sem], T.sem["lsent"], pid, rid, topo.mask(core, dst))
+        count["lsent"] = count.get("lsent", 0) + len(topo.engines(core, dst))
+        count[sem] = len(topo.engines(dst, core))
+        behind[(sem, count[sem])] = {}
+        writers.setdefault(land[0], []).append((land, (sem, count[sem]), "far"))
+
+    def u8(ap):
+        return ap.bitcast(dt.uint8)
+
+    def u32(ap):
+        return ap.bitcast(dt.uint32)
+
+    def gather_masked(win, winreg, tab, tabreg, mk="MK"):
+        op("V", lambda: v.tensor_tensor(T[mk][:], win.indirect(tab), T.MSK[:], A.mult), [winreg, tabreg, reg("MSK")], [reg(mk)])
+
+    def scan(mk="MK", sc="SC"):
+        op("V", lambda: v.tensor_tensor_scan(T[sc][:], T.NMS[:], T[mk][:], 0.0, A.mult, A.add), [reg(mk), reg("NMS")], [reg(sc)])
+
+    def sample(out, outreg, add, sc="SC"):
+        if add == 0.0:
+            op("V", lambda: v.tensor_copy(out, T[sc][:, 15:C:16]), [reg(sc)], [outreg])
+        else:
+            op("V", lambda: v.tensor_scalar(out, T[sc][:, 15:C:16], add, None, A.add), [reg(sc)], [outreg])
+
+    def gather_s(out, outreg, win, winreg, tab, tabreg):
+        op("S", lambda: s.activation(out, win.indirect(tab), COPY), [winreg, tabreg], [outreg])
+
+    def mm(bank, lq, ls, lo, rq, rs, start=True, stop=True):
+        b0 = 512 * bank
+        op("P", lambda: pe.matmul_mx(T.PS[:, b0:b0 + C], T[lq][:, lo:lo + 128], T[ls][:, lo:lo + 128], T[rq][:], T[rs][:], start, stop),
+           [reg(lq, lo, lo + 128), reg(ls, lo, lo + 128), reg(rq), reg(rs)], [reg("PS", b0, b0 + 512)])
+
+    def bank(b):
+        return reg("PS", 512 * b, 512 * b + 512)
+
+    def quant(q, sc, t):
+        op("V", lambda: v.quantize_mx(T[q][:], T[sc][:], T[t][:]), [reg(t)], [reg(q), reg(sc)])
+
+    dma("Y", T.X0[:], T.x[:], [], [reg("X0")])
+    dma("S", T.UT[:], T.u[:], [], [reg("UT")])
+    dma("Y", T.FLI[:], T.fl[:], [], [reg("FLI")])
+    dma("S", T.VT[:], T.v[:], [], [reg("VT")])
+    dma("Y", u8(T.WQ[:]), T.wc[:], [], [reg("WQ")])
+    dma("S", T.WS[:], T.ws[:], [], [reg("WS")])
+
+    op("G", lambda: g.iota(T.I1[:], [[1, C]], 128, -1), [], [reg("I1")])
+    op("G", lambda: g.iota(T.OI[:], [[16, 8]], 0, 0), [], [reg("OI")])
+    op("G", lambda: g.iota(T.PI[:], [[0, 20]], 0, 1), [], [reg("PI")])
+    op("G", lambda: g.iota(T.CI[:], [[16, 20]], -160, 0), [], [reg("CI")])
+    op("G", lambda: g.iota(T.IOS[:], [[1, C]], -160, 0, allow_small_or_imprecise_dtypes=True), [], [reg("IOS")])
+    op("V", lambda: v.memset(T.ET[:], 0.0), [], [reg("ET")])
+    op("V", lambda: v.tensor_scalar(T.IB[:], T.I1[:], 15, None, A.bitwise_and), [reg("I1")], [reg("IB")])
+    op("V", lambda: v.tensor_copy(T.UO[:], T.OI[:]), [reg("OI")], [reg("UO")])
+    op("V", lambda: v.tensor_scalar(T.MSK[:], T.IB[:], 0, None, A.is_equal), [reg("IB")], [reg("MSK")])
+    op("V", lambda: v.tensor_scalar(T.PK0[:, 0:20], T.FLI[:], -160.0, None, A.add), [reg("FLI")], [reg("PK0", 0, 20)])
+    send(T.cores[rank ^ MASK[0]], T.LP0[:, 0:20], T.PK0[:, 0:20], [reg("PK0", 0, 20)], reg("LP0", 0, 20), "apl")
+    for lo, hi, base, st in ((320, 416, 160, 1), (416, 544, 256, 2), (544, 640, 512, 4)):
+        op("G", lambda: g.iota(T.FW1[:, lo:hi], [[st, hi - lo]], base, 0, allow_small_or_imprecise_dtypes=True), [], [reg("FW1", lo, hi)])
+    quant("UQ", "US", "UT")
+    op("S", lambda: s.activation(T.US2[:], T.US[:].indirect(T.UO[:]), COPY), [reg("US"), reg("UO")], [reg("US2")])
+    op("V", lambda: v.tensor_copy(u32(T.UQ2[:]), u32(T.UQ[:]).indirect(T.UO[:])), [reg("UQ"), reg("UO")], [reg("UQ2")])
+    quant("QX0", "SX0", "X0")
+    for lo in range(C, FW2W, C):
+        n = min(C, FW2W - lo)
+        op("S", lambda: s.activation(T.FW2[:, lo:lo + n], T.IOS[:, 0:n], COPY), [reg("IOS")], [reg("FW2", lo, lo + n)])
+    for lo, hi, st, a0, a1 in ((416, 672, 2, 96, 224), (672, 1056, 4, 224, 320)):
+        op("S", lambda: s.activation(T.FW2[:, lo:hi:st], T.IOS[:, a0:a1], COPY), [reg("IOS")], [reg("FW2", lo, hi)])
+    op("V", lambda: v.tensor_scalar(T.NMS[:], T.MSK[:], 0.0, None, A.is_equal), [reg("MSK")], [reg("NMS")])
+    op("V", lambda: v.tensor_scalar(T.DG[:], T.I1[:, 0:128], 128, 0.5, A.is_equal, A.mult), [reg("I1")], [reg("DG")])
+    for b in range(4):
+        op("S", lambda: s.activation(T.ET[:, 512 * b + b:512 * b + 512:4], T.DG[:], COPY), [reg("DG")], [reg("ET", 512 * b, 512 * b + 512)])
+
+    def laid(r):
+        F4, PK, XF, X = ["%s%d" % (k, r) for k in ("F4", "PK", "XF", "X")]
+        for t in range(4):
+            op("V", lambda: v.tensor_scalar(T[F4][:, 20 * t:20 * t + 20], T[PK][:, 0:20], 4.0, 640.0 + t, A.mult, A.add),
+               [reg(PK, 0, 20)], [reg(F4, 20 * t, 20 * t + 20)])
+        for t in range(4):
+            gather_s(T[XF][:, t:4 * C:4], reg(XF, 0, 4 * C, t), T[X][:], reg(X), T[F4][:, 20 * t:20 * t + 20], reg(F4, 20 * t, 20 * t + 20))
+
+    for r, m in enumerate(MASK):
+        dst = T.cores[rank ^ m]
+        n_ = lambda k: k + str(r)
+        X, QX, SX, FS, FI, F4, PK, LP, LQ, LS = [n_(k) for k in ("X", "QX", "SX", "FS", "FI", "F4", "PK", "LP", "LQ", "LS")]
+        XF, QF, SF, F, M, Z, QZ, SZ, PW, WN, TB, TF, AT, AI, B3 = [n_(k) for k in ("XF", "QF", "SF", "F", "M", "Z", "QZ", "SZ", "PW", "WN", "TB", "TF", "AT", "AI", "B3")]
+        nxt = str(r + 1)
+
+        mm(4, "UQ2", "US2", 0, QX, SX)
+        if r == 0:
+            laid(0)
+        else:
+            ps = str(r - 1)
+            gather_masked(T["FS" + ps][:], reg("FS" + ps), T["AT" + ps][:], reg("AT" + ps), "MK2")
+            for b in range(4):
+                mm(b, "EQ", "ES", 128 * b, QX, SX)
+        op("V", lambda: v.tensor_tensor(T.MK[:], T.PS[:, 2048:2048 + C], T.MSK[:], A.mult), [bank(4), reg("MSK")], [reg("MK")])
+        if r > 0:
+            scan("MK2", "SC2")
+        else:
+            op("V", lambda: v.tensor_scalar(T.PA[:], T.PI[:], 15, None, A.bitwise_and), [reg("PI")], [reg("PA")])
+        scan()
+        if r > 0:
+            sample(T[PK][:, 0:20], reg(PK, 0, 20), 0.0, "SC2")
+        else:
+            op("V", lambda: v.tensor_tensor(T.ATS[:], T.PA[:], T.CI[:], A.add), [reg("PA"), reg("CI")], [reg("ATS")])
+        op("V", lambda: v.tensor_scalar(T[PK][:, 20:40], T.SC[:, 15:C:16], 0.0, None, A.is_gt), [reg("SC")], [reg(PK, 20, 40)])
+        if r == 0:
+            send(dst, T[LP][:, 20:40], T[PK][:, 20:40], [reg(PK, 20, 40)], reg(LP, 20, 40), n_("apk"))
+        else:
+            send(dst, T[LP][:], T[PK][:], [reg(PK)], reg(LP), n_("apk"))
+        send(dst, u8(T[LQ][:]), u8(T[QX][:]), [reg(QX)], reg(LQ), n_("aq"))
+        send(dst, T[LS][:], T[SX][:], [reg(SX)], reg(LS), n_("asc"))
+
+        if r > 0:
+            laid(r)
+        else:
+            quant("EQ", "ES", "ET")
+            for b in range(4):
+                mm(b, "EQ", "ES", 128 * b, QX, SX)
+            op("V", lambda: v.tensor_scalar(T.FT0[:], T[PK][:, 0:20], 160.0, None, A.add), [reg(PK, 0, 20)], [reg("FT0")])
+        for b in range(3):
+            if r == 0:
+                op("S", lambda: s.activation(T[F][:, C * b:C * b + C], T.PS[:, 512 * b:512 * b + C], COPY), [bank(b)], [reg(F, C * b, C * b + C)])
+            else:
+                op("V", lambda: v.tensor_copy(T[F][:, C * b:C * b + C], T.PS[:, 512 * b:512 * b + C]), [bank(b)], [reg(F, C * b, C * b + C)])
+        if r == 0:
+            op("V", lambda: v.tensor_copy(T.AI3[:].indirect(T.FT0[:]), T.IOS[:]), [reg("IOS"), reg("FT0")], [reg("AI3")])
+        quant(QF, SF, XF)
+        for b in range(4):
+            mm(4 + b, "EQ", "ES", 128 * b, QF, SF, True, False)
+        for b in range(4):
+            mm(4 + b, "EQ", "ES", 128 * b, LQ, LS, False, True)
+        if r == 0:
+            gather_s(T[FS][:], reg(FS), T.IOS[:], reg("IOS"), T.FT0[:], reg("FT0"))
+            op("V", lambda: v.tensor_tensor(T.MK[:], T.AI3[:], T.MSK[:], A.mult), [reg("AI3"), reg("MSK")], [reg("MK")])
+            scan()
+            sample(T[FI][:], reg(FI), 160.0)
+
+        def tf(i):
+            return T[TF][:, 20 * i:20 * i + 20]
+
+        def rf(i):
+            return reg(TF, 20 * i, 20 * i + 20)
+
+        def tb(i):
+            return T[TB][:, 20 * i:20 * i + 20]
+
+        def rb(i):
+            return reg(TB, 20 * i, 20 * i + 20)
+        es, be, le, lb = T[LP][:, 0:20], T[LP][:, 20:40], reg(LP, 0, 20), reg(LP, 20, 40)
+        op("V", lambda: v.tensor_tensor(tf(1), T.ATS[:], es, A.subtract), [le, reg("ATS")], [rf(1)])
+        op("V", lambda: v.tensor_tensor(tf(0), be, T[PK][:, 20:40], A.not_equal), [lb, reg(PK, 20, 40)], [rf(0)])
+        op("V", lambda: v.tensor_tensor(tf(2), tf(1), tf(0), A.mult), [rf(0), rf(1)], [rf(2)])
+        op("V", lambda: v.tensor_scalar(tf(4), tf(0), -320.0, 480.0, A.mult, A.add), [rf(0)], [rf(4)])
+        op("V", lambda: v.tensor_tensor(tf(3), tf(2), es, A.add), [rf(2), le], [rf(3)])
+        op("V", lambda: v.tensor_tensor(tf(5), T.ATS[:], tf(2), A.subtract), [rf(2), reg("ATS")], [rf(5)])
+        op("V", lambda: v.tensor_scalar(tb(0), tf(3), 160.0, None, A.add), [rf(3)], [rb(0)])
+
+        def slot(k):
+            return T[WN][:, C * k:C * k + C], reg(WN, C * k, C * k + C)
+        H = C // 2
+
+        def both(ob, lo, win, winreg, i):
+            t = T[TB]
+            op("V", lambda: v.tensor_copy(T[ob][:, lo:lo + H], win.indirect(t[:, 20 * i:20 * i + 10])), [winreg, rb(i)], [reg(ob, lo, lo + H)])
+            op("S", lambda: s.activation(T[ob][:, lo + H:lo + C], win.indirect(t[:, 20 * i + 10:20 * i + 20]), COPY), [winreg, rb(i)], [reg(ob, lo + H, lo + C)])
+            return T[ob][:, lo:lo + C], reg(ob, lo, lo + C)
+        w = both(WN, 0, T.IOS[:], reg("IOS"), 0)
+        op("V", lambda: v.tensor_tensor(tf(6), tf(5), tf(4), A.add), [rf(5), rf(4)], [rf(6)])
+
+        def evac_m(b):
+            op("S", lambda: s.activation(T[M][:, C * b:C * b + C], T.PS[:, 2048 + 512 * b:2048 + 512 * b + C], COPY), [bank(4 + b)], [reg(M, C * b, C * b + C)])
+        nslot, cur, pt, pw = 1, 0, 1, 1
+        for k, ahead in enumerate(STAGES):
+            for i in range(ahead):
+                w = both(WN, C * nslot, w[0], w[1], cur)
+                nslot, pw = nslot + 1, pw + pt
+            gather_masked(w[0], w[1], tb(cur), rb(cur))
+            w2 = slot(nslot)
+            gather_s(w2[0], w2[1], w[0], w[1], tb(cur), rb(cur))
+            nslot += 1
+            if k == 0:
+                op("V", lambda: v.tensor_copy(tb(1), tf(6)), [rf(6)], [rb(1)])
+            scan()
+            cur, w = k + 2, w2
+            pt, pw = pt + pw, pw + pt
+            sample(tb(cur), rb(cur), 160.0)
+            if k == len(STAGES) - 1:
+                evac_m(0)
+        for i in range(LAST):
+            ob, lo = ("FW1", 0) if i == LAST - 1 else (WN, C * nslot)
+            w = both(ob, lo, w[0], w[1], cur)
+            pw += pt
+        fin = len(STAGES) + 2
+        gather_masked(T.FW1[:], reg("FW1"), tb(1), rb(1))
+        gather_s(T.FW2[:, 0:C], reg("FW2", 0, C), w[0], w[1], tb(cur), rb(cur))
+        scan()
+        sample(tb(fin), rb(fin), 160.0)
+        assert pw + (pw + pt) >= C - 1
+        for b in range(1, 4):
+            evac_m(b)
+        gather_masked(T.FW2[:], reg("FW2"), tb(fin), rb(fin))
+        scan()
+        sample(T[AT][:], reg(AT), 160.0)
+
+        def plane(name, b):
+            return T[name][:, C * b:C * b + C], reg(name, C * b, C * b + C)
+        mw, mr = plane(M, 0)
+        op("V", lambda: v.tensor_copy(T[Z][:, 0:4 * C:4], mw.indirect(T[AT][:])), [mr, reg(AT)], [reg(Z, 0, 4 * C, 0)])
+        for b in range(1, 4):
+            mw, mr = plane(M, b)
+            gather_s(T[Z][:, b:4 * C:4], reg(Z, 0, 4 * C, b), mw, mr, T[AT][:], reg(AT))
+        op("V", lambda: v.tensor_copy(T[AI][:].indirect(T[AT][:]), T.IOS[:]), [reg("IOS"), reg(AT)], [reg(AI)])
+        quant(QZ, SZ, Z)
+        for b in range(4):
+            mm(4 + b, "WQ", "WS", 128 * b, QZ, SZ)
+        gather_s(T["FS" + nxt][:], reg("FS" + nxt), T[FS][:], reg(FS), T[AT][:], reg(AT))
+        gather_masked(T[AI][:], reg(AI), T[FI][:], reg(FI))
+        scan()
+        sample(T["FI" + nxt][:], reg("FI" + nxt), 160.0)
+        for b in range(4):
+            op("S", lambda: s.activation(T[PW][:, C * b:C * b + C], T.PS[:, 2048 + 512 * b:2048 + 512 * b + C], COPY, scale=0.015625),
+               [bank(4 + b)], [reg(PW, C * b, C * b + C)])
+        fi, fir = T["FI" + nxt][:], reg("FI" + nxt)
+        pw3, pr3 = plane(PW, 3)
+        gather_s(T[B3][:], reg(B3), pw3, pr3, fi, fir)
+        for b in range(3):
+            pw_, pr = plane(PW, b)
+            fw_, fr = plane(F, b)
+            op("V", lambda: v.tensor_tensor(T["X" + nxt][:, b:4 * C:4], pw_.indirect(fi), fw_, A.add),
+               [pr, fir, fr], [reg("X" + nxt, 0, 4 * C, b)])
+        op("V", lambda: v.tensor_tensor(T["X" + nxt][:, 3:4 * C:4], T[B3][:], T.PS[:, 1536:1536 + C], A.add),
+           [reg(B3), bank(3)], [reg("X" + nxt, 0, 4 * C, 3)])
+        quant("QX" + nxt, "SX" + nxt, "X" + nxt)
+        if r == 2:
+            quant("VQ", "VS", "VT")
+
+    mm(4, "VQ", "VS", 0, "QX3", "SX3")
+    dma("Y", T.oc[:], u8(T.QX3[:]), [reg("QX3")], [])
+    for k in range(4):
+        dma("Y" if k % 2 else "S", T.osc[4 * k:4 * k + 4, :], T.SX3[32 * k:32 * k + 4, :], [reg("SX3")], [])
+    op("V", lambda: v.tensor_scalar(T.LNF[:], T.FS3[:], 160.0, None, A.add), [reg("FS3")], [reg("LNF")])
+    op("V", lambda: v.tensor_copy(T.YS[:], T.PS[:, 2048:2048 + C]), [bank(4)], [reg("YS")])
+    dma("S", T.ln[:], T.LNF[0:128:16, :], [reg("LNF")], [])
+    dma("Y", T.y[:], T.YS[:], [reg("YS")], [])
+    for sem, val in count.items():
+        g.wait_ge(T.sem[sem], val)

@@ -1,32 +1,30 @@
 from concourse.mybir import dt, AluOpType, ActivationFunctionType
 
 C = 320
+H = C // 2
 MASK = [1, 2, 4]
-STAGES = [2, 2, 2]
-LAST = 1
-NW = 1 + sum(STAGES) + len(STAGES)
-FW2W = 1056
+RADIX = [4, 3, 3, 3, 3]
+NW = sum(RADIX) - len(RADIX)
+BIG = 2.0 ** 24
+OPT = {"path1": (0, 1), "xfv": 1, "scales_first": True}
 
 SCRATCH = {
-    "I1": ("sbuf", [128, C], "int32"), "IB": ("sbuf", [128, C], "int32"),
-    "IOS": ("sbuf", [128, C], "bfloat16"), "MSK": ("sbuf", [128, C], "bfloat16"), "NMS": ("sbuf", [128, C], "bfloat16"),
-    "PI": ("sbuf", [128, 20], "int32"), "CI": ("sbuf", [128, 20], "int32"), "PA": ("sbuf", [128, 20], "int32"),
-    "DG": ("sbuf", [128, 128], "bfloat16"),
-    "OI": ("sbuf", [128, 8], "int32"), "UO": ("sbuf", [128, 8], "uint16"),
-    "ATS": ("sbuf", [128, 20], "float32"),
-    "ET": ("sbuf", [128, 2048], "bfloat16"),
+    "Q16": ("sbuf", [128, 16], "int32"), "QA": ("sbuf", [128, 16], "int32"), "CI": ("sbuf", [128, 20], "int32"),
+    "PC": ("sbuf", [128, 8], "float32"), "CA": ("sbuf", [128, 32], "float32"), "C16": ("sbuf", [128, 16], "bfloat16"),
+    "PT": ("sbuf", [128, 20], "uint16"), "UO": ("sbuf", [128, 8], "uint16"),
+    "CSC": ("sbuf", [128, C], "bfloat16"), "J": ("sbuf", [128, 20], "float32"),
+    "IOS": ("sbuf", [128, C], "bfloat16"), "FW": ("sbuf", [128, 2 * C], "bfloat16"),
+    "ET": ("sbuf", [128, 520], "bfloat16"),
     "EQ": ("sbuf", [128, 512], "float8_e4m3fn_x4"), "ES": ("sbuf", [128, 512], "uint8"),
     "UT": ("sbuf", [128, 512], "bfloat16"), "VT": ("sbuf", [128, 512], "bfloat16"),
     "UQ": ("sbuf", [128, 128], "float8_e4m3fn_x4"), "US": ("sbuf", [128, 128], "uint8"),
     "UQ2": ("sbuf", [128, 128], "float8_e4m3fn_x4"), "US2": ("sbuf", [128, 128], "uint8"),
     "VQ": ("sbuf", [128, 128], "float8_e4m3fn_x4"), "VS": ("sbuf", [128, 128], "uint8"),
     "WQ": ("sbuf", [128, 512], "float8_e4m3fn_x4"), "WS": ("sbuf", [128, 512], "uint8"),
-    "FLI": ("sbuf", [128, 20], "int32"),
-    "AI3": ("sbuf", [128, C], "bfloat16"),
-    "FW1": ("sbuf", [128, 640], "bfloat16"), "FW2": ("sbuf", [128, FW2W], "bfloat16"),
-    "MK": ("sbuf", [128, C], "bfloat16"), "SC": ("sbuf", [128, C], "bfloat16"),
-    "MK2": ("sbuf", [128, C], "bfloat16"), "SC2": ("sbuf", [128, C], "bfloat16"),
-    "LNF": ("sbuf", [128, C], "float32"), "YS": ("sbuf", [128, C], "float32"),
+    "FLI": ("sbuf", [128, 20], "int32"), "FT0": ("sbuf", [128, 20], "uint16"),
+    "PL": ("sbuf", [128, 160], "float32"), "ST": ("sbuf", [128, 40], "float32"), "TF": ("sbuf", [128, 80], "float32"),
+    "SG": ("sbuf", [128, C], "bfloat16"), "SC": ("sbuf", [128, C], "bfloat16"), "SC2": ("sbuf", [128, C], "bfloat16"),
+    "LNF": ("sbuf", [128, C], "float32"), "YS": ("sbuf", [128, C], "float32"), "FI0S": ("sbuf", [128, C], "bfloat16"),
     "PS": ("psum", [128, 4096], "float32"),
 }
 for _r in range(4):
@@ -38,8 +36,9 @@ for _r in range(4):
     })
 for _r in range(3):
     SCRATCH.update({
-        "F4%d" % _r: ("sbuf", [128, 80], "uint16"),
-        "PK%d" % _r: ("sbuf", [128, 40], "bfloat16"), "LP%d" % _r: ("sbuf", [128, 40], "bfloat16"),
+        "F4%d" % _r: ("sbuf", [128, 80], "uint16"), "RT%d" % _r: ("sbuf", [128, 20], "uint16"),
+        "PK%d" % _r: ("sbuf", [128, 20], "bfloat16"), "LP%d" % _r: ("sbuf", [128, 20], "bfloat16"),
+        "LL%d" % _r: ("sbuf", [128, 40], "float32"),
         "LQ%d" % _r: ("sbuf", [128, C], "float8_e4m3fn_x4"), "LS%d" % _r: ("sbuf", [128, C], "uint8"),
         "XF%d" % _r: ("sbuf", [128, 4 * C], "bfloat16"),
         "QF%d" % _r: ("sbuf", [128, C], "float8_e4m3fn_x4"), "SF%d" % _r: ("sbuf", [128, C], "uint8"),
@@ -47,12 +46,11 @@ for _r in range(3):
         "Z%d" % _r: ("sbuf", [128, 4 * C], "bfloat16"),
         "QZ%d" % _r: ("sbuf", [128, C], "float8_e4m3fn_x4"), "SZ%d" % _r: ("sbuf", [128, C], "uint8"),
         "PW%d" % _r: ("sbuf", [128, 4 * C], "float32"), "B3%d" % _r: ("sbuf", [128, C], "float32"),
-        "WN%d" % _r: ("sbuf", [128, C * NW], "bfloat16"),
-        "TB%d" % _r: ("sbuf", [128, 20 * 12], "uint16"), "TF%d" % _r: ("sbuf", [128, 20 * 10], "float32"),
-        "AT%d" % _r: ("sbuf", [128, 20], "uint16"), "AI%d" % _r: ("sbuf", [128, C], "bfloat16"),
+        "WN%d" % _r: ("sbuf", [128, C * NW], "bfloat16"), "AS%d" % _r: ("sbuf", [128, C], "bfloat16"),
+        "TB%d" % _r: ("sbuf", [128, 20 * 8], "uint16"),
+        "AT%d" % _r: ("sbuf", [128, 20], "uint16"), "AI%d" % _r: ("sbuf", [128, C], "bfloat16"), "RI%d" % _r: ("sbuf", [128, C], "bfloat16"),
     })
-SCRATCH["FT0"] = ("sbuf", [128, 20], "uint16")
-SEMAPHORES = ["sV", "sS", "sP", "sG", "lsent", "apl"] + ["d%d" % i for i in range(16)] + [k + str(r) for r in range(3) for k in ("apk", "aq", "asc")]
+SEMAPHORES = ["sV", "sS", "sP", "sG", "lsent"] + ["d%d" % i for i in range(18)] + [k + str(r) for r in range(3) for k in ("al", "apk", "aq", "asc")]
 
 
 def rank_program(g, core, T, topo):
@@ -60,7 +58,8 @@ def rank_program(g, core, T, topo):
     if rank is None:
         return
     A = AluOpType
-    COPY = ActivationFunctionType.Copy
+    F_ = ActivationFunctionType
+    COPY = F_.Copy
     v, s, pe = g.vector, g.scalar, g.tensor
     queue = {"V": v, "S": s, "P": pe, "G": g, "Y": g.sync}
 
@@ -140,238 +139,277 @@ def rank_program(g, core, T, topo):
     def u32(ap):
         return ap.bitcast(dt.uint32)
 
-    def gather_masked(win, winreg, tab, tabreg, mk="MK"):
-        op("V", lambda: v.tensor_tensor(T[mk][:], win.indirect(tab), T.MSK[:], A.mult), [winreg, tabreg, reg("MSK")], [reg(mk)])
+    def ap(p):
+        return T[p[0]][:, p[1]:p[2]] if len(p) == 3 else T[p[0]][:, p[1]:p[2]:p[3]]
 
-    def scan(mk="MK", sc="SC"):
-        op("V", lambda: v.tensor_tensor_scan(T[sc][:], T.NMS[:], T[mk][:], 0.0, A.mult, A.add), [reg(mk), reg("NMS")], [reg(sc)])
+    def rg(p):
+        return reg(p[0], p[1], p[2]) if len(p) == 3 else reg(p[0], p[1] - p[1] % p[3], p[2], p[1] % p[3])
 
-    def sample(out, outreg, add, sc="SC"):
-        if add == 0.0:
-            op("V", lambda: v.tensor_copy(out, T[sc][:, 15:C:16]), [reg(sc)], [outreg])
+    def al(name):
+        return (name, 0, T[name].shape[1])
+
+    def ts(out, in0, s1, s2, op0, op1=None):
+        col = [x for x in (s1, s2) if isinstance(x, tuple)]
+        a1, a2 = [ap(x) if isinstance(x, tuple) else x for x in (s1, s2)]
+        more = [] if op1 is None else [op1]
+        op("V", lambda: v.tensor_scalar(ap(out), ap(in0), a1, a2, op0, *more), [rg(x) for x in [in0] + col], [rg(out)])
+
+    def tt(out, in0, in1, o):
+        op("V", lambda: v.tensor_tensor(ap(out), ap(in0), ap(in1), o), [rg(in0), rg(in1)], [rg(out)])
+
+    def cp(q, out, in_):
+        if q == "V":
+            op("V", lambda: v.tensor_copy(ap(out), ap(in_)), [rg(in_)], [rg(out)])
         else:
-            op("V", lambda: v.tensor_scalar(out, T[sc][:, 15:C:16], add, None, A.add), [reg(sc)], [outreg])
+            op("S", lambda: s.activation(ap(out), ap(in_), COPY), [rg(in_)], [rg(out)])
 
-    def gather_s(out, outreg, win, winreg, tab, tabreg):
-        op("S", lambda: s.activation(out, win.indirect(tab), COPY), [winreg, tabreg], [outreg])
+    def gather(q, out, win, tab):
+        if q == "V":
+            op("V", lambda: v.tensor_copy(ap(out), ap(win).indirect(ap(tab))), [rg(win), rg(tab)], [rg(out)])
+        else:
+            op("S", lambda: s.activation(ap(out), ap(win).indirect(ap(tab)), COPY), [rg(win), rg(tab)], [rg(out)])
 
-    def mm(bank, lq, ls, lo, rq, rs, start=True, stop=True):
-        b0 = 512 * bank
-        op("P", lambda: pe.matmul_mx(T.PS[:, b0:b0 + C], T[lq][:, lo:lo + 128], T[ls][:, lo:lo + 128], T[rq][:], T[rs][:], start, stop),
-           [reg(lq, lo, lo + 128), reg(ls, lo, lo + 128), reg(rq), reg(rs)], [reg("PS", b0, b0 + 512)])
+    def both(out, win, tab):
+        gather("V", (out[0], out[1], out[1] + H), win, (tab[0], tab[1], tab[1] + 10))
+        gather("S", (out[0], out[1] + H, out[2]), win, (tab[0], tab[1] + 10, tab[2]))
 
-    def bank(b):
+    def scatter(out, tab):
+        op("V", lambda: v.tensor_copy(ap(out).indirect(ap(tab)), ap(IOS)), [rg(IOS), rg(tab)], [rg(out)])
+
+    def scan(spread, sc="SC"):
+        op("V", lambda: v.tensor_tensor_scan(T[sc][:], T.CSC[:], ap(spread), 0.0, A.mult, A.add), [rg(spread), reg("CSC")], [reg(sc)])
+
+    def sample(out, sc="SC"):
+        ts(out, (sc, 15, C, 16), K, 160.25, A.mult, A.add)
+
+    def choose(out, pairs):
+        op("V", lambda: v.tensor_tensor_scan(ap(out), ap(OZ), ap(pairs), 0.0, A.mult, A.add), [rg(OZ), rg(pairs)], [rg(out)])
+
+    def bank(b, lo=0, n=C):
+        return ("PS", 512 * b + lo, 512 * b + lo + n)
+
+    def brg(b):
         return reg("PS", 512 * b, 512 * b + 512)
 
-    def quant(q, sc, t):
-        op("V", lambda: v.quantize_mx(T[q][:], T[sc][:], T[t][:]), [reg(t)], [reg(q), reg(sc)])
+    def evac(q, out, b, scale=None):
+        n = out[2] - out[1]
+        if q == "V":
+            op("V", lambda: v.tensor_copy(ap(out), ap(bank(b, 0, n))), [brg(b)], [rg(out)])
+        elif scale is None:
+            op("S", lambda: s.activation(ap(out), ap(bank(b, 0, n)), COPY), [brg(b)], [rg(out)])
+        else:
+            op("S", lambda: s.activation(ap(out), ap(bank(b, 0, n)), COPY, scale=scale), [brg(b)], [rg(out)])
 
-    dma("Y", T.X0[:], T.x[:], [], [reg("X0")])
-    dma("S", T.UT[:], T.u[:], [], [reg("UT")])
+    def mm(b, lq, ls, lo, rq, rs, start=True, stop=True, c0=0, c1=C):
+        op("P", lambda: pe.matmul_mx(ap(bank(b, 0, c1 - c0)), T[lq][:, lo:lo + 128], T[ls][:, lo:lo + 128], T[rq][:, c0:c1], T[rs][:, c0:c1], start, stop),
+           [reg(lq, lo, lo + 128), reg(ls, lo, lo + 128), reg(rq, c0, c1), reg(rs, c0, c1)], [brg(b)])
+
+    def quant(q, sc, t, c0=0, c1=None, at=None):
+        c1 = T[q].shape[1] if c1 is None else c1
+        at = 4 * c0 if at is None else at
+        op("V", lambda: v.quantize_mx(T[q][:, c0:c1], T[sc][:, c0:c1], T[t][:, at:at + 4 * (c1 - c0)]),
+           [reg(t, at, at + 4 * (c1 - c0))], [reg(q, c0, c1), reg(sc, c0, c1)])
+
+    def plane(name, b):
+        return (name, C * b, C * b + C)
+
+    def lane(name, b):
+        return (name, b, 4 * C, 4)
+
+    IOS = al("IOS")
+    PM, PF, K = ("PC", 0, 1), ("PC", 1, 2), ("PC", 2, 3)
+    OZ = ("PL", 120, 160)
+
+    def own(r):
+        return ("PL", 40 * r + 1, 40 * r + 40, 2)
+
+    def send_list(r):
+        send(T.cores[rank ^ MASK[r]], T["LL%d" % r][:], T.PL[:, 40 * r:40 * r + 40], [reg("PL", 40 * r, 40 * r + 40)], reg("LL%d" % r), "al%d" % r)
+
+    def offsets4(r):
+        for t in range(4):
+            ts(("F4%d" % r, 20 * t, 20 * t + 20), own(r), 4.0, t - 0.75, A.mult, A.add)
+
     dma("Y", T.FLI[:], T.fl[:], [], [reg("FLI")])
-    dma("S", T.VT[:], T.v[:], [], [reg("VT")])
-    dma("Y", u8(T.WQ[:]), T.wc[:], [], [reg("WQ")])
-    dma("S", T.WS[:], T.ws[:], [], [reg("WS")])
+    dma("S", T.UT[:], T.u[:], [], [reg("UT")])
+    dma("Y", T.X0[:, 0:2 * C], T.x[:, 0:2 * C], [], [reg("X0", 0, 2 * C)])
+    dma("S", T.X0[:, 2 * C:4 * C], T.x[:, 2 * C:4 * C], [], [reg("X0", 2 * C, 4 * C)])
 
-    op("G", lambda: g.iota(T.I1[:], [[1, C]], 128, -1), [], [reg("I1")])
-    op("G", lambda: g.iota(T.OI[:], [[16, 8]], 0, 0), [], [reg("OI")])
-    op("G", lambda: g.iota(T.PI[:], [[0, 20]], 0, 1), [], [reg("PI")])
-    op("G", lambda: g.iota(T.CI[:], [[16, 20]], -160, 0), [], [reg("CI")])
-    op("G", lambda: g.iota(T.IOS[:], [[1, C]], -160, 0, allow_small_or_imprecise_dtypes=True), [], [reg("IOS")])
+    op("G", lambda: g.iota(T.Q16[:], [[-1, 16]], 128, 1), [], [reg("Q16")])
+    op("G", lambda: g.iota(T.CI[:], [[16, 20]], 0, 0), [], [reg("CI")])
+    op("G", lambda: g.iota(ap(IOS), [[1, C]], -160, 0, allow_small_or_imprecise_dtypes=True), [], [rg(IOS)])
+    op("V", lambda: v.memset(T.PL[:], 0.0), [], [reg("PL")])
     op("V", lambda: v.memset(T.ET[:], 0.0), [], [reg("ET")])
-    op("V", lambda: v.tensor_scalar(T.IB[:], T.I1[:], 15, None, A.bitwise_and), [reg("I1")], [reg("IB")])
-    op("V", lambda: v.tensor_copy(T.UO[:], T.OI[:]), [reg("OI")], [reg("UO")])
-    op("V", lambda: v.tensor_scalar(T.MSK[:], T.IB[:], 0, None, A.is_equal), [reg("IB")], [reg("MSK")])
-    op("V", lambda: v.tensor_scalar(T.PK0[:, 0:20], T.FLI[:], -160.0, None, A.add), [reg("FLI")], [reg("PK0", 0, 20)])
-    send(T.cores[rank ^ MASK[0]], T.LP0[:, 0:20], T.PK0[:, 0:20], [reg("PK0", 0, 20)], reg("LP0", 0, 20), "apl")
-    for lo, hi, base, st in ((320, 416, 160, 1), (416, 544, 256, 2), (544, 640, 512, 4)):
-        op("G", lambda: g.iota(T.FW1[:, lo:hi], [[st, hi - lo]], base, 0, allow_small_or_imprecise_dtypes=True), [], [reg("FW1", lo, hi)])
+    ts(al("QA"), al("Q16"), 15, None, A.bitwise_and)
+    ts(PF, ("Q16", 0, 1), -288.0, None, A.add)
+    cp("V", al("UO"), ("CI", 0, 8))
+    cp("V", PM, ("QA", 0, 1))
+    ts(("CA", 0, 16), al("QA"), 15.0, BIG, A.is_equal, A.mult)
+    ts(("CA", 16, 32), al("QA"), 0.0, None, A.not_equal)
+    ts(al("PT"), al("CI"), 0.0, PM, A.mult, A.add)
+    tt(al("C16"), ("CA", 0, 16), ("CA", 16, 32), A.max)
+    gather("S", al("CSC"), al("C16"), al("PT"))
+    ts(K, ("QA", 0, 1), 15.0, 1.0 / BIG, A.is_equal, A.max)
+    ts(("ET", 3, 515, 4), ("IOS", 0, 128), PF, 0.5, A.is_equal, A.mult)
+    for b in range(2):
+        quant("EQ", "ES", "ET", 128 * b, 128 * b + 128, 3 - b)
+    ts(own(0), al("FLI"), 0.25, None, A.add)
+    send_list(0)
+    cp("V", al("FT0"), al("FLI"))
     quant("UQ", "US", "UT")
     op("S", lambda: s.activation(T.US2[:], T.US[:].indirect(T.UO[:]), COPY), [reg("US"), reg("UO")], [reg("US2")])
     op("V", lambda: v.tensor_copy(u32(T.UQ2[:]), u32(T.UQ[:]).indirect(T.UO[:])), [reg("UQ"), reg("UO")], [reg("UQ2")])
-    quant("QX0", "SX0", "X0")
-    for lo in range(C, FW2W, C):
-        n = min(C, FW2W - lo)
-        op("S", lambda: s.activation(T.FW2[:, lo:lo + n], T.IOS[:, 0:n], COPY), [reg("IOS")], [reg("FW2", lo, lo + n)])
-    for lo, hi, st, a0, a1 in ((416, 672, 2, 96, 224), (672, 1056, 4, 224, 320)):
-        op("S", lambda: s.activation(T.FW2[:, lo:hi:st], T.IOS[:, a0:a1], COPY), [reg("IOS")], [reg("FW2", lo, hi)])
-    op("V", lambda: v.tensor_scalar(T.NMS[:], T.MSK[:], 0.0, None, A.is_equal), [reg("MSK")], [reg("NMS")])
-    op("V", lambda: v.tensor_scalar(T.DG[:], T.I1[:, 0:128], 128, 0.5, A.is_equal, A.mult), [reg("I1")], [reg("DG")])
-    for b in range(4):
-        op("S", lambda: s.activation(T.ET[:, 512 * b + b:512 * b + 512:4], T.DG[:], COPY), [reg("DG")], [reg("ET", 512 * b, 512 * b + 512)])
-
-    def laid(r):
-        F4, PK, XF, X = ["%s%d" % (k, r) for k in ("F4", "PK", "XF", "X")]
-        for t in range(4):
-            op("V", lambda: v.tensor_scalar(T[F4][:, 20 * t:20 * t + 20], T[PK][:, 0:20], 4.0, 640.0 + t, A.mult, A.add),
-               [reg(PK, 0, 20)], [reg(F4, 20 * t, 20 * t + 20)])
-        for t in range(4):
-            gather_s(T[XF][:, t:4 * C:4], reg(XF, 0, 4 * C, t), T[X][:], reg(X), T[F4][:, 20 * t:20 * t + 20], reg(F4, 20 * t, 20 * t + 20))
+    gather("S", al("FS0"), IOS, al("FT0"))
+    cp("S", ("FW", C, 2 * C), IOS)
+    for b in range(2, 4):
+        quant("EQ", "ES", "ET", 128 * b, 128 * b + 128, 3 - b)
+    offsets4(0)
+    quant("QX0", "SX0", "X0", 0, H)
+    quant("QX0", "SX0", "X0", H, C)
 
     for r, m in enumerate(MASK):
         dst = T.cores[rank ^ m]
         n_ = lambda k: k + str(r)
-        X, QX, SX, FS, FI, F4, PK, LP, LQ, LS = [n_(k) for k in ("X", "QX", "SX", "FS", "FI", "F4", "PK", "LP", "LQ", "LS")]
-        XF, QF, SF, F, M, Z, QZ, SZ, PW, WN, TB, TF, AT, AI, B3 = [n_(k) for k in ("XF", "QF", "SF", "F", "M", "Z", "QZ", "SZ", "PW", "WN", "TB", "TF", "AT", "AI", "B3")]
+        X, QX, SX, FS, FI, F4, PK, LP, LL, LQ, LS = [n_(k) for k in ("X", "QX", "SX", "FS", "FI", "F4", "PK", "LP", "LL", "LQ", "LS")]
+        XF, QF, SF, F, M, Z, QZ, SZ, PW, WN, TB, AS, AT, AI, B3, RI, RT = [n_(k) for k in ("XF", "QF", "SF", "F", "M", "Z", "QZ", "SZ", "PW", "WN", "TB", "AS", "AT", "AI", "B3", "RI", "RT")]
         nxt = str(r + 1)
+        direct = r in OPT["path1"]
+        early4 = r == 0 or r - 1 in OPT["path1"]
 
-        mm(4, "UQ2", "US2", 0, QX, SX)
-        if r == 0:
-            laid(0)
-        else:
-            ps = str(r - 1)
-            gather_masked(T["FS" + ps][:], reg("FS" + ps), T["AT" + ps][:], reg("AT" + ps), "MK2")
-            for b in range(4):
-                mm(b, "EQ", "ES", 128 * b, QX, SX)
-        op("V", lambda: v.tensor_tensor(T.MK[:], T.PS[:, 2048:2048 + C], T.MSK[:], A.mult), [bank(4), reg("MSK")], [reg("MK")])
-        if r > 0:
-            scan("MK2", "SC2")
-        else:
-            op("V", lambda: v.tensor_scalar(T.PA[:], T.PI[:], 15, None, A.bitwise_and), [reg("PI")], [reg("PA")])
-        scan()
-        if r > 0:
-            sample(T[PK][:, 0:20], reg(PK, 0, 20), 0.0, "SC2")
-        else:
-            op("V", lambda: v.tensor_tensor(T.ATS[:], T.PA[:], T.CI[:], A.add), [reg("PA"), reg("CI")], [reg("ATS")])
-        op("V", lambda: v.tensor_scalar(T[PK][:, 20:40], T.SC[:, 15:C:16], 0.0, None, A.is_gt), [reg("SC")], [reg(PK, 20, 40)])
-        if r == 0:
-            send(dst, T[LP][:, 20:40], T[PK][:, 20:40], [reg(PK, 20, 40)], reg(LP, 20, 40), n_("apk"))
-        else:
-            send(dst, T[LP][:], T[PK][:], [reg(PK)], reg(LP), n_("apk"))
-        send(dst, u8(T[LQ][:]), u8(T[QX][:]), [reg(QX)], reg(LQ), n_("aq"))
-        send(dst, T[LS][:], T[SX][:], [reg(SX)], reg(LS), n_("asc"))
-
-        if r > 0:
-            laid(r)
-        else:
-            quant("EQ", "ES", "ET")
-            for b in range(4):
-                mm(b, "EQ", "ES", 128 * b, QX, SX)
-            op("V", lambda: v.tensor_scalar(T.FT0[:], T[PK][:, 0:20], 160.0, None, A.add), [reg(PK, 0, 20)], [reg("FT0")])
-        for b in range(3):
-            if r == 0:
-                op("S", lambda: s.activation(T[F][:, C * b:C * b + C], T.PS[:, 512 * b:512 * b + C], COPY), [bank(b)], [reg(F, C * b, C * b + C)])
+        mm(4, "UQ2", "US2", 0, QX, SX, c0=0, c1=H)
+        mm(5, "UQ2", "US2", 0, QX, SX, c0=H, c1=C)
+        for b in range(4):
+            mm(b, "EQ", "ES", 128 * b, QX, SX)
+        if not early4:
+            scan(al(FS), "SC2")
+            sample(own(r), "SC2")
+            send_list(r)
+        if OPT["scales_first"]:
+            send(dst, T[LS][:], T[SX][:], [reg(SX)], reg(LS), n_("asc"))
+        if early4 and r > 0:
+            gather("S", lane(XF, 3), al(X), (F4, 60, 80))
+        first, second = ("S", "V") if r == 0 else ("V", "S")
+        for q, b, lo in ((first, 4, 0), (second, 5, H)):
+            if q == "S":
+                op("S", lambda: s.activation(T.SG[:, lo:lo + H], ap(bank(b, 0, H)), F_.Sign, bias=-2.0 ** -93), [brg(b)], [reg("SG", lo, lo + H)])
             else:
-                op("V", lambda: v.tensor_copy(T[F][:, C * b:C * b + C], T.PS[:, 512 * b:512 * b + C]), [bank(b)], [reg(F, C * b, C * b + C)])
+                op("V", lambda: v.tensor_scalar(T.SG[:, lo:lo + H], ap(bank(b, 0, H)), 0.0, None, A.is_gt), [brg(b)], [reg("SG", lo, lo + H)])
+        scan(al("SG"))
+        ts(al(PK), ("SC", 15, C, 16), K, 0.5, A.mult, A.is_gt)
+        send(dst, T[LP][:], T[PK][:], [reg(PK)], reg(LP), n_("apk"))
+        if not OPT["scales_first"]:
+            send(dst, T[LS][:], T[SX][:], [reg(SX)], reg(LS), n_("asc"))
+        send(dst, u8(T[LQ][:]), u8(T[QX][:]), [reg(QX)], reg(LQ), n_("aq"))
         if r == 0:
-            op("V", lambda: v.tensor_copy(T.AI3[:].indirect(T.FT0[:]), T.IOS[:]), [reg("IOS"), reg("FT0")], [reg("AI3")])
+            dma("Y", u8(T.WQ[:]), T.wc[:], [reg(LQ)], [reg("WQ")])
+            dma("Y", T.WS[:], T.ws[:], [], [reg("WS")])
+            dma("Y", T.VT[:], T.v[:], [], [reg("VT")])
+
+        if not early4:
+            evac("S", plane(F, 0), 0)
+            evac("S", plane(F, 1), 1)
+            offsets4(r)
+        if r == 0:
+            ts(al("J"), al("CI"), PM, 0.25, A.add, A.add)
+            ts(("ST", 1, 40, 2), al("CI"), PM, 320.25, A.add, A.add)
+        for t in range(3 if early4 and r > 0 else 4):
+            gather("V" if t < OPT["xfv"] else "S", lane(XF, t), al(X), (F4, 20 * t, 20 * t + 20))
+        if early4:
+            evac("V", plane(F, 0), 0)
+            evac("V" if r == 0 else "S", plane(F, 1), 1)
+        if r == 0 and not direct:
+            scatter(al("FI0S"), al("FT0"))
+            scan(al("FI0S"))
+            sample(al(FI))
+        tt((LL, 0, 40, 2), al("J"), (LL, 1, 40, 2), A.subtract)
+        ts(("ST", 0, 40, 2), (LL, 0, 40, 2), -1.0, -320.0, A.mult, A.add)
         quant(QF, SF, XF)
         for b in range(4):
             mm(4 + b, "EQ", "ES", 128 * b, QF, SF, True, False)
         for b in range(4):
             mm(4 + b, "EQ", "ES", 128 * b, LQ, LS, False, True)
-        if r == 0:
-            gather_s(T[FS][:], reg(FS), T.IOS[:], reg("IOS"), T.FT0[:], reg("FT0"))
-            op("V", lambda: v.tensor_tensor(T.MK[:], T.AI3[:], T.MSK[:], A.mult), [reg("AI3"), reg("MSK")], [reg("MK")])
-            scan()
-            sample(T[FI][:], reg(FI), 160.0)
-
-        def tf(i):
-            return T[TF][:, 20 * i:20 * i + 20]
-
-        def rf(i):
-            return reg(TF, 20 * i, 20 * i + 20)
 
         def tb(i):
-            return T[TB][:, 20 * i:20 * i + 20]
+            return (TB, 20 * i, 20 * i + 20)
+        tt(("PL", 121, 160, 2), al(LP), al(PK), A.not_equal)
+        choose(("TF", 0, 40), al(LL))
+        cp("V", tb(0), ("TF", 1, 40, 2))
+        w = (WN, 0, C)
+        both(w, IOS, tb(0))
+        choose(("TF", 40, 80), al("ST"))
+        spare = [lambda: evac("S", plane(F, 2), 2)] + [lambda b=b: evac("S", plane(M, b), 4 + b) for b in range(4)]
+        nslot, cur, reach = 1, 0, 1
+        for k, radix in enumerate(RADIX):
+            last = k == len(RADIX) - 1
+            for i in range(radix - 1):
+                w2 = ("FW", 0, C) if last and i == radix - 2 else (WN, C * nslot, C * nslot + C)
+                both(w2, w, tb(cur))
+                if k == 0 and i == 0:
+                    cp("V", tb(1), ("TF", 41, 80, 2))
+                w, nslot = w2, nslot + 1
+            reach *= radix
+            if not last:
+                scan(w)
+                cur = k + 2
+                sample(tb(cur))
+                spare.pop(0)()
+        assert reach >= C - 1
+        both(al(AS), al("FW"), tb(1))
+        scan(al(AS))
+        sample(al(AT))
+        while spare:
+            spare.pop(0)()
 
-        def rb(i):
-            return reg(TB, 20 * i, 20 * i + 20)
-        es, be, le, lb = T[LP][:, 0:20], T[LP][:, 20:40], reg(LP, 0, 20), reg(LP, 20, 40)
-        op("V", lambda: v.tensor_tensor(tf(1), T.ATS[:], es, A.subtract), [le, reg("ATS")], [rf(1)])
-        op("V", lambda: v.tensor_tensor(tf(0), be, T[PK][:, 20:40], A.not_equal), [lb, reg(PK, 20, 40)], [rf(0)])
-        op("V", lambda: v.tensor_tensor(tf(2), tf(1), tf(0), A.mult), [rf(0), rf(1)], [rf(2)])
-        op("V", lambda: v.tensor_scalar(tf(4), tf(0), -320.0, 480.0, A.mult, A.add), [rf(0)], [rf(4)])
-        op("V", lambda: v.tensor_tensor(tf(3), tf(2), es, A.add), [rf(2), le], [rf(3)])
-        op("V", lambda: v.tensor_tensor(tf(5), T.ATS[:], tf(2), A.subtract), [rf(2), reg("ATS")], [rf(5)])
-        op("V", lambda: v.tensor_scalar(tb(0), tf(3), 160.0, None, A.add), [rf(3)], [rb(0)])
-
-        def slot(k):
-            return T[WN][:, C * k:C * k + C], reg(WN, C * k, C * k + C)
-        H = C // 2
-
-        def both(ob, lo, win, winreg, i):
-            t = T[TB]
-            op("V", lambda: v.tensor_copy(T[ob][:, lo:lo + H], win.indirect(t[:, 20 * i:20 * i + 10])), [winreg, rb(i)], [reg(ob, lo, lo + H)])
-            op("S", lambda: s.activation(T[ob][:, lo + H:lo + C], win.indirect(t[:, 20 * i + 10:20 * i + 20]), COPY), [winreg, rb(i)], [reg(ob, lo + H, lo + C)])
-            return T[ob][:, lo:lo + C], reg(ob, lo, lo + C)
-        w = both(WN, 0, T.IOS[:], reg("IOS"), 0)
-        op("V", lambda: v.tensor_tensor(tf(6), tf(5), tf(4), A.add), [rf(5), rf(4)], [rf(6)])
-
-        def evac_m(b):
-            op("S", lambda: s.activation(T[M][:, C * b:C * b + C], T.PS[:, 2048 + 512 * b:2048 + 512 * b + C], COPY), [bank(4 + b)], [reg(M, C * b, C * b + C)])
-        nslot, cur, pt, pw = 1, 0, 1, 1
-        for k, ahead in enumerate(STAGES):
-            for i in range(ahead):
-                w = both(WN, C * nslot, w[0], w[1], cur)
-                nslot, pw = nslot + 1, pw + pt
-            gather_masked(w[0], w[1], tb(cur), rb(cur))
-            w2 = slot(nslot)
-            gather_s(w2[0], w2[1], w[0], w[1], tb(cur), rb(cur))
-            nslot += 1
-            if k == 0:
-                op("V", lambda: v.tensor_copy(tb(1), tf(6)), [rf(6)], [rb(1)])
-            scan()
-            cur, w = k + 2, w2
-            pt, pw = pt + pw, pw + pt
-            sample(tb(cur), rb(cur), 160.0)
-            if k == len(STAGES) - 1:
-                evac_m(0)
-        for i in range(LAST):
-            ob, lo = ("FW1", 0) if i == LAST - 1 else (WN, C * nslot)
-            w = both(ob, lo, w[0], w[1], cur)
-            pw += pt
-        fin = len(STAGES) + 2
-        gather_masked(T.FW1[:], reg("FW1"), tb(1), rb(1))
-        gather_s(T.FW2[:, 0:C], reg("FW2", 0, C), w[0], w[1], tb(cur), rb(cur))
-        scan()
-        sample(tb(fin), rb(fin), 160.0)
-        assert pw + (pw + pt) >= C - 1
-        for b in range(1, 4):
-            evac_m(b)
-        gather_masked(T.FW2[:], reg("FW2"), tb(fin), rb(fin))
-        scan()
-        sample(T[AT][:], reg(AT), 160.0)
-
-        def plane(name, b):
-            return T[name][:, C * b:C * b + C], reg(name, C * b, C * b + C)
-        mw, mr = plane(M, 0)
-        op("V", lambda: v.tensor_copy(T[Z][:, 0:4 * C:4], mw.indirect(T[AT][:])), [mr, reg(AT)], [reg(Z, 0, 4 * C, 0)])
-        for b in range(1, 4):
-            mw, mr = plane(M, b)
-            gather_s(T[Z][:, b:4 * C:4], reg(Z, 0, 4 * C, b), mw, mr, T[AT][:], reg(AT))
-        op("V", lambda: v.tensor_copy(T[AI][:].indirect(T[AT][:]), T.IOS[:]), [reg("IOS"), reg(AT)], [reg(AI)])
-        quant(QZ, SZ, Z)
+        fi = al("FI" + nxt)
+        if direct:
+            gather("S", al("FS" + nxt), al(FS), al(AT))
+            gather("V", lane(Z, 0), plane(M, 0), al(AT))
+            for b in range(1, 4):
+                gather("S", lane(Z, b), plane(M, b), al(AT))
+            scan(al("FS" + nxt), "SC2")
+            sample(al(RT), "SC2")
+            scatter(al(RI), al(RT))
+            quant(QZ, SZ, Z)
+            scan(al(RI))
+            sample(fi)
+            if r < 2:
+                sample(own(r + 1), "SC2")
+                send_list(r + 1)
+                offsets4(r + 1)
+        else:
+            scatter(al(AI), al(AT))
+            for b in range(3):
+                gather("S", lane(Z, b), plane(M, b), al(AT))
+            gather("V", lane(Z, 3), plane(M, 3), al(AT))
+            gather("S", al(RI), al(AI), al(FI))
+            quant(QZ, SZ, Z)
+            scan(al(RI))
+            sample(fi)
         for b in range(4):
             mm(4 + b, "WQ", "WS", 128 * b, QZ, SZ)
-        gather_s(T["FS" + nxt][:], reg("FS" + nxt), T[FS][:], reg(FS), T[AT][:], reg(AT))
-        gather_masked(T[AI][:], reg(AI), T[FI][:], reg(FI))
-        scan()
-        sample(T["FI" + nxt][:], reg("FI" + nxt), 160.0)
         for b in range(4):
-            op("S", lambda: s.activation(T[PW][:, C * b:C * b + C], T.PS[:, 2048 + 512 * b:2048 + 512 * b + C], COPY, scale=0.015625),
-               [bank(4 + b)], [reg(PW, C * b, C * b + C)])
-        fi, fir = T["FI" + nxt][:], reg("FI" + nxt)
-        pw3, pr3 = plane(PW, 3)
-        gather_s(T[B3][:], reg(B3), pw3, pr3, fi, fir)
+            evac("S", plane(PW, b), 4 + b, 0.015625)
+        gather("S", al(B3), plane(PW, 3), fi)
         for b in range(3):
-            pw_, pr = plane(PW, b)
-            fw_, fr = plane(F, b)
-            op("V", lambda: v.tensor_tensor(T["X" + nxt][:, b:4 * C:4], pw_.indirect(fi), fw_, A.add),
-               [pr, fir, fr], [reg("X" + nxt, 0, 4 * C, b)])
-        op("V", lambda: v.tensor_tensor(T["X" + nxt][:, 3:4 * C:4], T[B3][:], T.PS[:, 1536:1536 + C], A.add),
-           [reg(B3), bank(3)], [reg("X" + nxt, 0, 4 * C, 3)])
-        quant("QX" + nxt, "SX" + nxt, "X" + nxt)
+            op("V", lambda: v.tensor_tensor(ap(lane("X" + nxt, b)), ap(plane(PW, b)).indirect(ap(fi)), ap(plane(F, b)), A.add),
+               [rg(plane(PW, b)), rg(fi), rg(plane(F, b))], [rg(lane("X" + nxt, b))])
+        op("V", lambda: v.tensor_tensor(ap(lane("X" + nxt, 3)), T[B3][:], ap(bank(3)), A.add), [reg(B3), brg(3)], [rg(lane("X" + nxt, 3))])
+        if r < 2 and not direct:
+            gather("S", al("FS" + nxt), al(FS), al(AT))
         if r == 2:
+            op("S", lambda: s.activation(T.LNF[:], T[FS][:].indirect(T[AT][:]), F_.Identity, bias=160.0), [reg(FS), reg(AT)], [reg("LNF")])
+            dma("Y", T.ln[:], T.LNF[0:128:16, :], [reg("LNF")], [])
+        quant("QX" + nxt, "SX" + nxt, "X" + nxt)
+        if r == 0:
             quant("VQ", "VS", "VT")
 
-    mm(4, "VQ", "VS", 0, "QX3", "SX3")
+    mm(4, "VQ", "VS", 0, "QX3", "SX3", c0=0, c1=H)
+    mm(5, "VQ", "VS", 0, "QX3", "SX3", c0=H, c1=C)
     dma("Y", T.oc[:], u8(T.QX3[:]), [reg("QX3")], [])
     for k in range(4):
-        dma("Y" if k % 2 else "S", T.osc[4 * k:4 * k + 4, :], T.SX3[32 * k:32 * k + 4, :], [reg("SX3")], [])
-    op("V", lambda: v.tensor_scalar(T.LNF[:], T.FS3[:], 160.0, None, A.add), [reg("FS3")], [reg("LNF")])
-    op("V", lambda: v.tensor_copy(T.YS[:], T.PS[:, 2048:2048 + C]), [bank(4)], [reg("YS")])
-    dma("S", T.ln[:], T.LNF[0:128:16, :], [reg("LNF")], [])
-    dma("Y", T.y[:], T.YS[:], [reg("YS")], [])
+        dma("Y", T.osc[4 * k:4 * k + 4, :], T.SX3[32 * k:32 * k + 4, :], [reg("SX3")], [])
+    evac("V", ("YS", 0, H), 4)
+    evac("S", ("YS", H, C), 5)
+    dma("S", T.y[:], T.YS[:], [reg("YS")], [])
     for sem, val in count.items():
         g.wait_ge(T.sem[sem], val)

@@ -2,11 +2,12 @@ from concourse.mybir import dt, AluOpType, ActivationFunctionType
 
 C = 320
 H = C // 2
+CUT = ((0, H), (H, C))
 MASK = [1, 2, 4]
-RADIX = [4, 3, 3, 3, 3]
-NW = sum(RADIX) - len(RADIX)
+STEPS = "g g tg g g tg g g tg g g t g g".split()
+NW = len(STEPS)
+AHEAD = 18
 BIG = 2.0 ** 24
-OPT = {"path1": (0, 1), "xfv": 1, "scales_first": True}
 
 SCRATCH = {
     "Q16": ("sbuf", [128, 16], "int32"), "QA": ("sbuf", [128, 16], "int32"), "CI": ("sbuf", [128, 20], "int32"),
@@ -21,36 +22,34 @@ SCRATCH = {
     "UQ2": ("sbuf", [128, 128], "float8_e4m3fn_x4"), "US2": ("sbuf", [128, 128], "uint8"),
     "VQ": ("sbuf", [128, 128], "float8_e4m3fn_x4"), "VS": ("sbuf", [128, 128], "uint8"),
     "WQ": ("sbuf", [128, 512], "float8_e4m3fn_x4"), "WS": ("sbuf", [128, 512], "uint8"),
-    "FLI": ("sbuf", [128, 20], "int32"), "FT0": ("sbuf", [128, 20], "uint16"),
-    "PL": ("sbuf", [128, 160], "float32"), "ST": ("sbuf", [128, 40], "float32"), "TF": ("sbuf", [128, 80], "float32"),
+    "FLI": ("sbuf", [128, 20], "int32"), "LI": ("sbuf", [128, 20], "int32"), "FT0": ("sbuf", [128, 20], "uint16"),
+    "PL": ("sbuf", [128, 120], "float32"), "PK": ("sbuf", [128, 120], "bfloat16"),
+    "AB": ("sbuf", [128, 80], "float32"), "SN": ("sbuf", [128, 20], "float32"), "TF": ("sbuf", [128, 80], "float32"),
     "SG": ("sbuf", [128, C], "bfloat16"), "SC": ("sbuf", [128, C], "bfloat16"), "SC2": ("sbuf", [128, C], "bfloat16"),
-    "LNF": ("sbuf", [128, C], "float32"), "YS": ("sbuf", [128, C], "float32"), "FI0S": ("sbuf", [128, C], "bfloat16"),
+    "AI": ("sbuf", [128, C], "bfloat16"),
+    "LNF": ("sbuf", [128, C], "float32"), "YS": ("sbuf", [128, C], "float32"),
+    "QX3": ("sbuf", [128, C], "float8_e4m3fn_x4"), "SX3": ("sbuf", [128, C], "uint8"), "X3": ("sbuf", [128, 4 * C], "bfloat16"),
     "PS": ("psum", [128, 4096], "float32"),
 }
-for _r in range(4):
+for _r in range(3):
     SCRATCH.update({
         "X%d" % _r: ("sbuf", [128, 4 * C], "bfloat16"),
         "QX%d" % _r: ("sbuf", [128, C], "float8_e4m3fn_x4"), "SX%d" % _r: ("sbuf", [128, C], "uint8"),
-        "FS%d" % _r: ("sbuf", [128, C], "bfloat16"),
-        "FI%d" % _r: ("sbuf", [128, 20], "uint16"),
-    })
-for _r in range(3):
-    SCRATCH.update({
+        "FS%d" % _r: ("sbuf", [128, C], "bfloat16"), "FI%d" % _r: ("sbuf", [128, 20], "uint16"),
         "F4%d" % _r: ("sbuf", [128, 80], "uint16"), "RT%d" % _r: ("sbuf", [128, 20], "uint16"),
-        "PK%d" % _r: ("sbuf", [128, 20], "bfloat16"), "LP%d" % _r: ("sbuf", [128, 20], "bfloat16"),
-        "LL%d" % _r: ("sbuf", [128, 40], "float32"),
+        "B3%d" % _r: ("sbuf", [128, C], "float32"), "LP%d" % _r: ("sbuf", [128, 40], "bfloat16"), "LL%d" % _r: ("sbuf", [128, 80], "float32"),
         "LQ%d" % _r: ("sbuf", [128, C], "float8_e4m3fn_x4"), "LS%d" % _r: ("sbuf", [128, C], "uint8"),
         "XF%d" % _r: ("sbuf", [128, 4 * C], "bfloat16"),
         "QF%d" % _r: ("sbuf", [128, C], "float8_e4m3fn_x4"), "SF%d" % _r: ("sbuf", [128, C], "uint8"),
         "F%d" % _r: ("sbuf", [128, 3 * C], "bfloat16"), "M%d" % _r: ("sbuf", [128, 4 * C], "bfloat16"),
         "Z%d" % _r: ("sbuf", [128, 4 * C], "bfloat16"),
         "QZ%d" % _r: ("sbuf", [128, C], "float8_e4m3fn_x4"), "SZ%d" % _r: ("sbuf", [128, C], "uint8"),
-        "PW%d" % _r: ("sbuf", [128, 4 * C], "float32"), "B3%d" % _r: ("sbuf", [128, C], "float32"),
+        "PW%d" % _r: ("sbuf", [128, 4 * C], "float32"),
         "WN%d" % _r: ("sbuf", [128, C * NW], "bfloat16"), "AS%d" % _r: ("sbuf", [128, C], "bfloat16"),
         "TB%d" % _r: ("sbuf", [128, 20 * 8], "uint16"),
-        "AT%d" % _r: ("sbuf", [128, 20], "uint16"), "AI%d" % _r: ("sbuf", [128, C], "bfloat16"), "RI%d" % _r: ("sbuf", [128, C], "bfloat16"),
+        "AT%d" % _r: ("sbuf", [128, 20], "uint16"), "RI%d" % _r: ("sbuf", [128, C], "bfloat16"),
     })
-SEMAPHORES = ["sV", "sS", "sP", "sG", "lsent"] + ["d%d" % i for i in range(18)] + [k + str(r) for r in range(3) for k in ("al", "apk", "aq", "asc")]
+SEMAPHORES = ["sV", "sS", "sP", "sG", "lsent", "out"] + ["d%d" % i for i in range(7)] + [k + str(r) for r in range(3) for k in ("al", "apk", "aq", "asc")]
 
 
 def rank_program(g, core, T, topo):
@@ -116,11 +115,12 @@ def rank_program(g, core, T, topo):
 
     ndma = [0]
 
-    def dma(q, out, in_, rd, wr):
+    def dma(q, out, in_, rd, wr, sem=None):
         deps(q, rd, wr, True)
-        sem = "d%d" % ndma[0]
-        ndma[0] += 1
-        count[sem] = 16
+        if sem is None:
+            sem = "d%d" % ndma[0]
+            ndma[0] += 1
+        count[sem] = count.get(sem, 0) + 16
         queue[q].dma_start(out, in_).then_inc(T.sem[sem], 16)
         note(q, rd, wr, (sem, 16), "dma" + sem)
 
@@ -169,21 +169,33 @@ def rank_program(g, core, T, topo):
         else:
             op("S", lambda: s.activation(ap(out), ap(win).indirect(ap(tab)), COPY), [rg(win), rg(tab)], [rg(out)])
 
-    def both(out, win, tab):
-        gather("V", (out[0], out[1], out[1] + H), win, (tab[0], tab[1], tab[1] + 10))
-        gather("S", (out[0], out[1] + H, out[2]), win, (tab[0], tab[1] + 10, tab[2]))
+    def both(out, win, tab, k):
+        st = out[3] if len(out) == 4 else 1
+        gather("V", (out[0], out[1], out[1] + 16 * k * st - out[1] % st) + out[3:], win, (tab[0], tab[1], tab[1] + k))
+        if k < 20:
+            gather("S", (out[0], out[1] + 16 * k * st, out[2]) + out[3:], win, (tab[0], tab[1] + k, tab[2]))
 
-    def scatter(out, tab):
-        op("V", lambda: v.tensor_copy(ap(out).indirect(ap(tab)), ap(IOS)), [rg(IOS), rg(tab)], [rg(out)])
+    def scatter(out, tab, lo=0, hi=20):
+        op("V", lambda: v.tensor_copy(ap(out).indirect(T[tab[0]][:, lo:hi]), T.IOS[:, 16 * lo:16 * hi]), [rg(IOS), rg(tab)], [rg(out)])
 
     def scan(spread, sc="SC"):
-        op("V", lambda: v.tensor_tensor_scan(T[sc][:], T.CSC[:], ap(spread), 0.0, A.mult, A.add), [rg(spread), reg("CSC")], [reg(sc)])
+        lo = spread[1] % C
+        hi = lo + spread[2] - spread[1]
+        op("V", lambda: v.tensor_tensor_scan(T[sc][:, lo:hi], T.CSC[:, lo:hi], ap(spread), 0.0, A.mult, A.add), [rg(spread), reg("CSC")], [reg(sc, lo, hi)])
+
+    def held(sc="SC"):
+        return (sc, 15, C, 16)
 
     def sample(out, sc="SC"):
-        ts(out, (sc, 15, C, 16), K, 160.25, A.mult, A.add)
+        ts(out, held(sc), K, 160.25, A.mult, A.add)
 
-    def choose(out, pairs):
-        op("V", lambda: v.tensor_tensor_scan(ap(out), ap(OZ), ap(pairs), 0.0, A.mult, A.add), [rg(OZ), rg(pairs)], [rg(out)])
+    def table(out, w, k):
+        scan((w[0], w[1], w[1] + 16 * k))
+        scan((w[0], w[1] + 16 * k, w[2]))
+        sample(out)
+
+    def choose(out, bits, pairs):
+        op("V", lambda: v.tensor_tensor_scan(ap(out), ap(bits), ap(pairs), 0.0, A.mult, A.add), [rg(bits), rg(pairs)], [rg(out)])
 
     def bank(b, lo=0, n=C):
         return ("PS", 512 * b + lo, 512 * b + lo + n)
@@ -218,28 +230,28 @@ def rank_program(g, core, T, topo):
 
     IOS = al("IOS")
     PM, PF, K = ("PC", 0, 1), ("PC", 1, 2), ("PC", 2, 3)
-    OZ = ("PL", 120, 160)
 
     def own(r):
         return ("PL", 40 * r + 1, 40 * r + 40, 2)
 
     def send_list(r):
-        send(T.cores[rank ^ MASK[r]], T["LL%d" % r][:], T.PL[:, 40 * r:40 * r + 40], [reg("PL", 40 * r, 40 * r + 40)], reg("LL%d" % r), "al%d" % r)
+        send(T.cores[rank ^ MASK[r]], T["LL%d" % r][:, 0:40], T.PL[:, 40 * r:40 * r + 40], [reg("PL", 40 * r, 40 * r + 40)], reg("LL%d" % r, 0, 40), "al%d" % r)
 
-    def offsets4(r):
-        for t in range(4):
+    def offsets4(r, which):
+        for t in which:
             ts(("F4%d" % r, 20 * t, 20 * t + 20), own(r), 4.0, t - 0.75, A.mult, A.add)
 
     dma("Y", T.FLI[:], T.fl[:], [], [reg("FLI")])
     dma("S", T.UT[:], T.u[:], [], [reg("UT")])
-    dma("Y", T.X0[:, 0:2 * C], T.x[:, 0:2 * C], [], [reg("X0", 0, 2 * C)])
-    dma("S", T.X0[:, 2 * C:4 * C], T.x[:, 2 * C:4 * C], [], [reg("X0", 2 * C, 4 * C)])
+    for q, (lo, hi) in zip("YS", CUT):
+        dma(q, T.X0[:, 4 * lo:4 * hi], T.x[:, 4 * lo:4 * hi], [], [reg("X0", 4 * lo, 4 * hi)])
 
     op("G", lambda: g.iota(T.Q16[:], [[-1, 16]], 128, 1), [], [reg("Q16")])
     op("G", lambda: g.iota(T.CI[:], [[16, 20]], 0, 0), [], [reg("CI")])
     op("G", lambda: g.iota(ap(IOS), [[1, C]], -160, 0, allow_small_or_imprecise_dtypes=True), [], [rg(IOS)])
-    op("V", lambda: v.memset(T.PL[:], 0.0), [], [reg("PL")])
-    op("V", lambda: v.memset(T.ET[:], 0.0), [], [reg("ET")])
+    send(T.cores[rank ^ MASK[0]], T.LI[:], T.FLI[:], [reg("FLI")], reg("LI"), "al0")
+    for name in ("PL", "PK", "ET"):
+        op("V", lambda: v.memset(T[name][:], 0.0), [], [reg(name)])
     ts(al("QA"), al("Q16"), 15, None, A.bitwise_and)
     ts(PF, ("Q16", 0, 1), -288.0, None, A.add)
     cp("V", al("UO"), ("CI", 0, 8))
@@ -248,168 +260,179 @@ def rank_program(g, core, T, topo):
     ts(("CA", 16, 32), al("QA"), 0.0, None, A.not_equal)
     ts(al("PT"), al("CI"), 0.0, PM, A.mult, A.add)
     tt(al("C16"), ("CA", 0, 16), ("CA", 16, 32), A.max)
+    cp("S", ("FW", C, 2 * C), IOS)
     gather("S", al("CSC"), al("C16"), al("PT"))
     ts(K, ("QA", 0, 1), 15.0, 1.0 / BIG, A.is_equal, A.max)
     ts(("ET", 3, 515, 4), ("IOS", 0, 128), PF, 0.5, A.is_equal, A.mult)
-    for b in range(2):
+    ts(al("J"), al("CI"), PM, 0.25, A.add, A.add)
+
+    def eq(b):
         quant("EQ", "ES", "ET", 128 * b, 128 * b + 128, 3 - b)
-    ts(own(0), al("FLI"), 0.25, None, A.add)
-    send_list(0)
-    cp("V", al("FT0"), al("FLI"))
+    eq(0)
+    eq(1)
     quant("UQ", "US", "UT")
+    eq(2)
     op("S", lambda: s.activation(T.US2[:], T.US[:].indirect(T.UO[:]), COPY), [reg("US"), reg("UO")], [reg("US2")])
     op("V", lambda: v.tensor_copy(u32(T.UQ2[:]), u32(T.UQ[:]).indirect(T.UO[:])), [reg("UQ"), reg("UO")], [reg("UQ2")])
-    gather("S", al("FS0"), IOS, al("FT0"))
-    cp("S", ("FW", C, 2 * C), IOS)
-    for b in range(2, 4):
-        quant("EQ", "ES", "ET", 128 * b, 128 * b + 128, 3 - b)
-    offsets4(0)
-    quant("QX0", "SX0", "X0", 0, H)
-    quant("QX0", "SX0", "X0", H, C)
+    ts(own(0), al("FLI"), 0.25, None, A.add)
+    quant("QX0", "SX0", "X0", *CUT[0])
+    offsets4(0, (3, 2))
+    quant("QX0", "SX0", "X0", *CUT[1])
+    for r in range(3):
+        op("S", lambda: s.activation(T["LL%d" % r][:, 41:80:2], T.J[:], F_.Identity, bias=320.0), [reg("J")], [rg(("LL%d" % r, 41, 80, 2))])
 
     for r, m in enumerate(MASK):
         dst = T.cores[rank ^ m]
         n_ = lambda k: k + str(r)
-        X, QX, SX, FS, FI, F4, PK, LP, LL, LQ, LS = [n_(k) for k in ("X", "QX", "SX", "FS", "FI", "F4", "PK", "LP", "LL", "LQ", "LS")]
-        XF, QF, SF, F, M, Z, QZ, SZ, PW, WN, TB, AS, AT, AI, B3, RI, RT = [n_(k) for k in ("XF", "QF", "SF", "F", "M", "Z", "QZ", "SZ", "PW", "WN", "TB", "AS", "AT", "AI", "B3", "RI", "RT")]
+        X, QX, SX, FS, FI, F4, B3, LP, LL, LQ, LS = [n_(k) for k in ("X", "QX", "SX", "FS", "FI", "F4", "B3", "LP", "LL", "LQ", "LS")]
+        XF, QF, SF, F, M, Z, QZ, SZ, PW, WN, TB, AS, AT, RI, RT = [n_(k) for k in ("XF", "QF", "SF", "F", "M", "Z", "QZ", "SZ", "PW", "WN", "TB", "AS", "AT", "RI", "RT")]
         nxt = str(r + 1)
-        direct = r in OPT["path1"]
-        early4 = r == 0 or r - 1 in OPT["path1"]
 
-        mm(4, "UQ2", "US2", 0, QX, SX, c0=0, c1=H)
-        mm(5, "UQ2", "US2", 0, QX, SX, c0=H, c1=C)
-        for b in range(4):
-            mm(b, "EQ", "ES", 128 * b, QX, SX)
-        if not early4:
-            scan(al(FS), "SC2")
-            sample(own(r), "SC2")
-            send_list(r)
-        if OPT["scales_first"]:
-            send(dst, T[LS][:], T[SX][:], [reg(SX)], reg(LS), n_("asc"))
-        if early4 and r > 0:
-            gather("S", lane(XF, 3), al(X), (F4, 60, 80))
-        first, second = ("S", "V") if r == 0 else ("V", "S")
-        for q, b, lo in ((first, 4, 0), (second, 5, H)):
-            if q == "S":
-                op("S", lambda: s.activation(T.SG[:, lo:lo + H], ap(bank(b, 0, H)), F_.Sign, bias=-2.0 ** -93), [brg(b)], [reg("SG", lo, lo + H)])
-            else:
-                op("V", lambda: v.tensor_scalar(T.SG[:, lo:lo + H], ap(bank(b, 0, H)), 0.0, None, A.is_gt), [brg(b)], [reg("SG", lo, lo + H)])
-        scan(al("SG"))
-        ts(al(PK), ("SC", 15, C, 16), K, 0.5, A.mult, A.is_gt)
-        send(dst, T[LP][:], T[PK][:], [reg(PK)], reg(LP), n_("apk"))
-        if not OPT["scales_first"]:
-            send(dst, T[LS][:], T[SX][:], [reg(SX)], reg(LS), n_("asc"))
+        for i, (lo, hi) in enumerate(CUT):
+            mm(4 + i, "UQ2", "US2", 0, QX, SX, c0=lo, c1=hi)
+        if r > 0:
+            for b in range(4):
+                mm(b, "EQ", "ES", 128 * b, QX, SX)
+        gather("S", lane(XF, 3), al(X), (F4, 60, 80))
+        offsets4(r, (1, 0))
+        op("V", lambda: v.tensor_scalar(T.SG[:, 0:H], ap(bank(4, 0, H)), 0.0, None, A.is_gt), [brg(4)], [reg("SG", 0, H)])
+        op("S", lambda: s.activation(T.SG[:, H:C], ap(bank(5, 0, H)), F_.Sign, bias=-2.0 ** -93), [brg(5)], [reg("SG", H, C)])
+        for lo, hi in CUT:
+            scan(("SG", lo, hi))
+        bits = ("PK", 40 * r, 40 * r + 40)
+        mine = ("PK", 40 * r + 1, 40 * r + 40, 2)
+        ts(mine, held(), K, 0.5, A.mult, A.is_gt)
+        send(dst, T[LP][:], ap(bits), [rg(bits)], reg(LP), n_("apk"))
+        send(dst, T[LS][:], T[SX][:], [reg(SX)], reg(LS), n_("asc"))
         send(dst, u8(T[LQ][:]), u8(T[QX][:]), [reg(QX)], reg(LQ), n_("aq"))
         if r == 0:
+            eq(3)
+            cp("V", al("FT0"), al("FLI"))
+            for b in range(4):
+                mm(b, "EQ", "ES", 128 * b, QX, SX)
             dma("Y", u8(T.WQ[:]), T.wc[:], [reg(LQ)], [reg("WQ")])
             dma("Y", T.WS[:], T.ws[:], [], [reg("WS")])
             dma("Y", T.VT[:], T.v[:], [], [reg("VT")])
 
-        if not early4:
-            evac("S", plane(F, 0), 0)
-            evac("S", plane(F, 1), 1)
-            offsets4(r)
+        for t in (2, 1):
+            gather("S", lane(XF, t), al(X), (F4, 20 * t, 20 * t + 20))
+        gather("V", lane(XF, 0), al(X), (F4, 0, 20))
         if r == 0:
-            ts(al("J"), al("CI"), PM, 0.25, A.add, A.add)
-            ts(("ST", 1, 40, 2), al("CI"), PM, 320.25, A.add, A.add)
-        for t in range(3 if early4 and r > 0 else 4):
-            gather("V" if t < OPT["xfv"] else "S", lane(XF, t), al(X), (F4, 20 * t, 20 * t + 20))
-        if early4:
-            evac("V", plane(F, 0), 0)
-            evac("V" if r == 0 else "S", plane(F, 1), 1)
-        if r == 0 and not direct:
-            scatter(al("FI0S"), al("FT0"))
-            scan(al("FI0S"))
-            sample(al(FI))
+            ts((LL, 1, 40, 2), al("LI"), 0.25, None, A.add)
+        ts(al("SN"), mine, -2.0, 1.0, A.mult, A.add)
         tt((LL, 0, 40, 2), al("J"), (LL, 1, 40, 2), A.subtract)
-        ts(("ST", 0, 40, 2), (LL, 0, 40, 2), -1.0, -320.0, A.mult, A.add)
-        quant(QF, SF, XF)
-        for b in range(4):
-            mm(4 + b, "EQ", "ES", 128 * b, QF, SF, True, False)
-        for b in range(4):
-            mm(4 + b, "EQ", "ES", 128 * b, LQ, LS, False, True)
+        tt((LL, 40, 80, 2), (LL, 1, 40, 2), (LL, 41, 80, 2), A.subtract)
+        for lo in (0, 40):
+            choose(("AB", lo, lo + 40), bits, (LL, lo, lo + 40))
+        for lo in (0, 40):
+            tt(("AB", lo, lo + 40, 2), (LL, lo, lo + 40, 2), al("SN"), A.mult)
+        for b in range(3):
+            evac("S", plane(F, b), b)
+        if r == 0:
+            gather("S", al("FS0"), IOS, al("FT0"))
 
         def tb(i):
             return (TB, 20 * i, 20 * i + 20)
-        tt(("PL", 121, 160, 2), al(LP), al(PK), A.not_equal)
-        choose(("TF", 0, 40), al(LL))
-        cp("V", tb(0), ("TF", 1, 40, 2))
+        for i in range(2):
+            choose(("TF", 40 * i, 40 * i + 40), al(LP), ("AB", 40 * i, 40 * i + 40))
+        for i in range(2):
+            cp("V", tb(i), ("TF", 40 * i + 1, 40 * i + 40, 2))
         w = (WN, 0, C)
-        both(w, IOS, tb(0))
-        choose(("TF", 40, 80), al("ST"))
-        spare = [lambda: evac("S", plane(F, 2), 2)] + [lambda b=b: evac("S", plane(M, b), 4 + b) for b in range(4)]
-        nslot, cur, reach = 1, 0, 1
-        for k, radix in enumerate(RADIX):
-            last = k == len(RADIX) - 1
-            for i in range(radix - 1):
-                w2 = ("FW", 0, C) if last and i == radix - 2 else (WN, C * nslot, C * nslot + C)
-                both(w2, w, tb(cur))
-                if k == 0 and i == 0:
-                    cp("V", tb(1), ("TF", 41, 80, 2))
-                w, nslot = w2, nslot + 1
-            reach *= radix
-            if not last:
+        both(w, IOS, tb(0), 10)
+        quant(QF, SF, XF, *CUT[0])
+        cur, pt, pw = 0, 1, 1
+        for k, step in enumerate(STEPS):
+            w2 = ("FW", 0, C) if k == len(STEPS) - 1 else (WN, C * k + C, C * k + 2 * C)
+            if step == "g":
+                both(w2, w, tb(cur), 10)
+                w, pw = w2, pw + pt
+            else:
                 scan(w)
-                cur = k + 2
+                if step == "tg":
+                    both(w2, w, tb(cur), 4)
+                cur = max(cur + 1, 2)
                 sample(tb(cur))
-                spare.pop(0)()
-        assert reach >= C - 1
-        both(al(AS), al("FW"), tb(1))
+                if step == "tg":
+                    w, pt, pw = w2, pw, pw + pt
+                else:
+                    pt = pw
+                    for b in range(2):
+                        evac("S", plane(M, b), 4 + b)
+            if k == 0:
+                quant(QF, SF, XF, *CUT[1])
+                for b in range(4):
+                    mm(4 + b, "EQ", "ES", 128 * b, QF, SF, True, False)
+                for b in range(4):
+                    mm(4 + b, "EQ", "ES", 128 * b, LQ, LS, False, True)
+        assert pw >= C - 1
+        both(al(AS), al("FW"), tb(1), 10)
         scan(al(AS))
         sample(al(AT))
-        while spare:
-            spare.pop(0)()
+        for b in range(2, 4):
+            evac("S", plane(M, b), 4 + b)
 
-        fi = al("FI" + nxt)
-        if direct:
-            gather("S", al("FS" + nxt), al(FS), al(AT))
-            gather("V", lane(Z, 0), plane(M, 0), al(AT))
-            for b in range(1, 4):
+        fi = al(FI)
+        if r < 2:
+            def piece(q, lo, hi):
+                gather(q, (Z, 64 * lo + 3, 64 * hi, 4), plane(M, 3), (AT, lo, hi))
+            both(al("FS" + nxt), al(FS), al(AT), 10)
+            piece("V", 0, 4)
+            for b in range(3):
                 gather("S", lane(Z, b), plane(M, b), al(AT))
             scan(al("FS" + nxt), "SC2")
+            piece("V", 4, 8)
             sample(al(RT), "SC2")
-            scatter(al(RI), al(RT))
-            quant(QZ, SZ, Z)
-            scan(al(RI))
-            sample(fi)
-            if r < 2:
-                sample(own(r + 1), "SC2")
-                send_list(r + 1)
-                offsets4(r + 1)
+            piece("V", 8, 12)
+            piece("S", 12, 20)
+            scatter(al(RI), al(RT), 0, AHEAD)
+            op("S", lambda: s.activation(ap(own(r + 1)), ap(held("SC2")), F_.Identity, bias=160.25, scale=ap(K)), [rg(held("SC2")), rg(K)], [rg(own(r + 1))])
+            send_list(r + 1)
         else:
-            scatter(al(AI), al(AT))
+            scatter(al("AI"), al(AT))
             for b in range(3):
                 gather("S", lane(Z, b), plane(M, b), al(AT))
             gather("V", lane(Z, 3), plane(M, 3), al(AT))
-            gather("S", al(RI), al(AI), al(FI))
-            quant(QZ, SZ, Z)
-            scan(al(RI))
-            sample(fi)
-        for b in range(4):
+            gather("S", al(RI), al("AI"), al("FI%d" % (r - 1)))
+        for lo, hi in CUT:
+            quant(QZ, SZ, Z, lo, hi)
+        if r < 2:
+            scatter(al(RI), al(RT), AHEAD, 20)
+        if r == 1:
+            quant("VQ", "VS", "VT")
+        scan(al(RI))
+        if r < 2:
+            offsets4(r + 1, (3,))
+        sample(fi)
+        if r < 2:
+            offsets4(r + 1, (2,))
+        mm(0, "WQ", "WS", 0, QZ, SZ, c0=0, c1=H)
+        mm(4, "WQ", "WS", 0, QZ, SZ, c0=H, c1=C)
+        for b in (1, 3, 2):
             mm(4 + b, "WQ", "WS", 128 * b, QZ, SZ)
-        for b in range(4):
+        evac("S", (PW, 0, H), 0, 0.015625)
+        evac("S", (PW, H, C), 4, 0.015625)
+        for b in (1, 3, 2):
             evac("S", plane(PW, b), 4 + b, 0.015625)
         gather("S", al(B3), plane(PW, 3), fi)
         for b in range(3):
             op("V", lambda: v.tensor_tensor(ap(lane("X" + nxt, b)), ap(plane(PW, b)).indirect(ap(fi)), ap(plane(F, b)), A.add),
                [rg(plane(PW, b)), rg(fi), rg(plane(F, b))], [rg(lane("X" + nxt, b))])
-        op("V", lambda: v.tensor_tensor(ap(lane("X" + nxt, 3)), T[B3][:], ap(bank(3)), A.add), [reg(B3), brg(3)], [rg(lane("X" + nxt, 3))])
-        if r < 2 and not direct:
-            gather("S", al("FS" + nxt), al(FS), al(AT))
+        for lo, hi in CUT:
+            out = ("X" + nxt, 4 * lo + 3, 4 * hi, 4)
+            op("V", lambda: v.tensor_tensor(ap(out), T[B3][:, lo:hi], ap(bank(3, lo, hi - lo)), A.add), [reg(B3), brg(3)], [rg(out)])
+        for lo, hi in CUT:
+            quant("QX" + nxt, "SX" + nxt, "X" + nxt, lo, hi)
         if r == 2:
             op("S", lambda: s.activation(T.LNF[:], T[FS][:].indirect(T[AT][:]), F_.Identity, bias=160.0), [reg(FS), reg(AT)], [reg("LNF")])
-            dma("Y", T.ln[:], T.LNF[0:128:16, :], [reg("LNF")], [])
-        quant("QX" + nxt, "SX" + nxt, "X" + nxt)
-        if r == 0:
-            quant("VQ", "VS", "VT")
+            dma("S", T.ln[:], T.LNF[0:128:16, :], [reg("LNF")], [], "out")
 
-    mm(4, "VQ", "VS", 0, "QX3", "SX3", c0=0, c1=H)
-    mm(5, "VQ", "VS", 0, "QX3", "SX3", c0=H, c1=C)
-    dma("Y", T.oc[:], u8(T.QX3[:]), [reg("QX3")], [])
+    for i, (lo, hi) in enumerate(CUT):
+        mm(4 + i, "VQ", "VS", 0, "QX3", "SX3", c0=lo, c1=hi)
+    dma("Y", T.oc[:], u8(T.QX3[:]), [reg("QX3")], [], "out")
+    evac("V", ("YS",) + CUT[0], 4)
+    evac("S", ("YS",) + CUT[1], 5)
+    dma("S", T.y[:], T.YS[:], [reg("YS")], [], "out")
     for k in range(4):
-        dma("Y", T.osc[4 * k:4 * k + 4, :], T.SX3[32 * k:32 * k + 4, :], [reg("SX3")], [])
-    evac("V", ("YS", 0, H), 4)
-    evac("S", ("YS", H, C), 5)
-    dma("S", T.y[:], T.YS[:], [reg("YS")], [])
-    for sem, val in count.items():
-        g.wait_ge(T.sem[sem], val)
+        dma("YYYS"[k], T.osc[4 * k:4 * k + 4, :], T.SX3[32 * k:32 * k + 4, :], [reg("SX3")], [], "out")
+    for sem in sorted(count, key=lambda k: (k == "out", k in ("sP", "sV", "sS"))):
+        g.wait_ge(T.sem[sem], count[sem])

@@ -4,17 +4,27 @@ C = 320
 H = C // 2
 CUT = ((0, H), (H, C))
 MASK = [1, 2, 4]
-STEPS = "g g tg g g tg g g tg g g t g g".split()
-NW = len(STEPS)
+STEPS = "g tg g tg g tg tg g tg g".split()
+NW = len(STEPS) + 2
+BIG = 2.0 ** 40
+PIECE = 80
+ZV = 18
+TGV = (4, 4, 4, 4, 4, 4, 4)
+FEV = 3
+QGAP = 0
+MV = [(0, 0, 80), (0, 80, 160), (0, 160, 240), (0, 240, 320), (3, 0, 80), (3, 80, 160)]
+MS = [(1, 0, 80), (1, 80, 160), (1, 160, 240), (1, 240, 320)]
+MEND = [(2, 0, 320), (3, 160, 320)]
 AHEAD = 18
-BIG = 2.0 ** 24
 
 SCRATCH = {
     "Q16": ("sbuf", [128, 16], "int32"), "QA": ("sbuf", [128, 16], "int32"), "CI": ("sbuf", [128, 20], "int32"),
     "PC": ("sbuf", [128, 8], "float32"), "CA": ("sbuf", [128, 32], "float32"), "C16": ("sbuf", [128, 16], "bfloat16"),
     "PT": ("sbuf", [128, 20], "uint16"), "UO": ("sbuf", [128, 8], "uint16"),
-    "CSC": ("sbuf", [128, C], "bfloat16"), "J": ("sbuf", [128, 20], "float32"),
-    "IOS": ("sbuf", [128, C], "bfloat16"), "FW": ("sbuf", [128, 2 * C], "bfloat16"),
+    "CSC": ("sbuf", [128, C], "bfloat16"), "J": ("sbuf", [128, 60], "float32"), "KS": ("sbuf", [128, 60], "float32"),
+    "FAR": ("sbuf", [128, 40], "float32"),
+    "IOS": ("sbuf", [128, C], "bfloat16"), "FW": ("sbuf", [128, 768], "bfloat16"),
+    "WK": ("sbuf", [128, 2 * C], "bfloat16"), "AW": ("sbuf", [128, C], "bfloat16"),
     "ET": ("sbuf", [128, 520], "bfloat16"),
     "EQ": ("sbuf", [128, 512], "float8_e4m3fn_x4"), "ES": ("sbuf", [128, 512], "uint8"),
     "UT": ("sbuf", [128, 512], "bfloat16"), "VT": ("sbuf", [128, 512], "bfloat16"),
@@ -23,10 +33,11 @@ SCRATCH = {
     "VQ": ("sbuf", [128, 128], "float8_e4m3fn_x4"), "VS": ("sbuf", [128, 128], "uint8"),
     "WQ": ("sbuf", [128, 512], "float8_e4m3fn_x4"), "WS": ("sbuf", [128, 512], "uint8"),
     "FLI": ("sbuf", [128, 20], "int32"), "LI": ("sbuf", [128, 20], "int32"), "FT0": ("sbuf", [128, 20], "uint16"),
-    "PL": ("sbuf", [128, 120], "float32"), "PK": ("sbuf", [128, 120], "bfloat16"),
-    "AB": ("sbuf", [128, 80], "float32"), "SN": ("sbuf", [128, 20], "float32"), "TF": ("sbuf", [128, 80], "float32"),
-    "SG": ("sbuf", [128, C], "bfloat16"), "SC": ("sbuf", [128, C], "bfloat16"), "SC2": ("sbuf", [128, C], "bfloat16"),
-    "AI": ("sbuf", [128, C], "bfloat16"),
+    "OL": ("sbuf", [128, 60], "float32"), "DL": ("sbuf", [128, 40], "float32"),
+    "PP": ("sbuf", [128, 160], "float32"), "BB": ("sbuf", [128, 240], "bfloat16"), "TF": ("sbuf", [128, 120], "float32"),
+    "SG": ("sbuf", [128, C], "bfloat16"), "SC": ("sbuf", [128, C], "bfloat16"), "SC2": ("sbuf", [128, C], "bfloat16"), "SC3": ("sbuf", [128, C], "bfloat16"), "SCS": ("sbuf", [128, C], "bfloat16"),
+    "AI": ("sbuf", [128, C], "bfloat16"), "RI": ("sbuf", [128, C], "bfloat16"), "FI": ("sbuf", [128, 80], "uint16"),
+    "LP0": ("sbuf", [128, 40], "bfloat16"), "LP1": ("sbuf", [128, 40], "float32"), "LP2": ("sbuf", [128, 40], "float32"),
     "LNF": ("sbuf", [128, C], "float32"), "YS": ("sbuf", [128, C], "float32"),
     "QX3": ("sbuf", [128, C], "float8_e4m3fn_x4"), "SX3": ("sbuf", [128, C], "uint8"), "X3": ("sbuf", [128, 4 * C], "bfloat16"),
     "PS": ("psum", [128, 4096], "float32"),
@@ -35,9 +46,8 @@ for _r in range(3):
     SCRATCH.update({
         "X%d" % _r: ("sbuf", [128, 4 * C], "bfloat16"),
         "QX%d" % _r: ("sbuf", [128, C], "float8_e4m3fn_x4"), "SX%d" % _r: ("sbuf", [128, C], "uint8"),
-        "FS%d" % _r: ("sbuf", [128, C], "bfloat16"), "FI%d" % _r: ("sbuf", [128, 20], "uint16"),
-        "F4%d" % _r: ("sbuf", [128, 80], "uint16"), "RT%d" % _r: ("sbuf", [128, 20], "uint16"),
-        "B3%d" % _r: ("sbuf", [128, C], "float32"), "LP%d" % _r: ("sbuf", [128, 40], "bfloat16"), "LL%d" % _r: ("sbuf", [128, 80], "float32"),
+        "FS%d" % _r: ("sbuf", [128, C], "bfloat16"),
+        "F4%d" % _r: ("sbuf", [128, 80], "uint16"), "B3%d" % _r: ("sbuf", [128, C], "float32"),
         "LQ%d" % _r: ("sbuf", [128, C], "float8_e4m3fn_x4"), "LS%d" % _r: ("sbuf", [128, C], "uint8"),
         "XF%d" % _r: ("sbuf", [128, 4 * C], "bfloat16"),
         "QF%d" % _r: ("sbuf", [128, C], "float8_e4m3fn_x4"), "SF%d" % _r: ("sbuf", [128, C], "uint8"),
@@ -46,10 +56,9 @@ for _r in range(3):
         "QZ%d" % _r: ("sbuf", [128, C], "float8_e4m3fn_x4"), "SZ%d" % _r: ("sbuf", [128, C], "uint8"),
         "PW%d" % _r: ("sbuf", [128, 4 * C], "float32"),
         "WN%d" % _r: ("sbuf", [128, C * NW], "bfloat16"), "AS%d" % _r: ("sbuf", [128, C], "bfloat16"),
-        "TB%d" % _r: ("sbuf", [128, 20 * 8], "uint16"),
-        "AT%d" % _r: ("sbuf", [128, 20], "uint16"), "RI%d" % _r: ("sbuf", [128, C], "bfloat16"),
+        "TB%d" % _r: ("sbuf", [128, 20 * 10], "uint16"), "AT%d" % _r: ("sbuf", [128, 20], "uint16"),
     })
-SEMAPHORES = ["sV", "sS", "sP", "sG", "lsent", "out"] + ["d%d" % i for i in range(7)] + [k + str(r) for r in range(3) for k in ("al", "apk", "aq", "asc")]
+SEMAPHORES = ["sV", "sS", "sP", "sG", "lsent", "out", "al0"] + ["d%d" % i for i in range(7)] + [k + str(r) for r in range(3) for k in ("apk", "aq", "asc")]
 
 
 def rank_program(g, core, T, topo):
@@ -94,9 +103,11 @@ def rank_program(g, core, T, topo):
         toks = []
         for r_ in rd:
             toks += [t for (x, t, e) in writers.get(r_[0], []) if meet(x, r_)]
+            if r_[0] == "PS":
+                toks += [t for (x, t, e) in readers.get("PS", []) if meet(x, r_) and e != q]
         for w_ in wr:
             toks += [t for (x, t, e) in writers.get(w_[0], []) if meet(x, w_) and not (q == "P" and e == q)]
-            toks += [t for (x, t, e) in readers.get(w_[0], []) if meet(x, w_) and (dma or e != q)]
+            toks += [t for (x, t, e) in readers.get(w_[0], []) if meet(x, w_) and not (q == "P" and e == q)]
         need(q, toks)
 
     def note(q, rd, wr, tok, e):
@@ -148,6 +159,15 @@ def rank_program(g, core, T, topo):
     def al(name):
         return (name, 0, T[name].shape[1])
 
+    def part(name, i, n=20):
+        return (name, n * i, n * i + n)
+
+    def even(p):
+        return (p[0], p[1], p[2], 2)
+
+    def odd(p):
+        return (p[0], p[1] + 1, p[2], 2)
+
     def ts(out, in0, s1, s2, op0, op1=None):
         col = [x for x in (s1, s2) if isinstance(x, tuple)]
         a1, a2 = [ap(x) if isinstance(x, tuple) else x for x in (s1, s2)]
@@ -156,6 +176,9 @@ def rank_program(g, core, T, topo):
 
     def tt(out, in0, in1, o):
         op("V", lambda: v.tensor_tensor(ap(out), ap(in0), ap(in1), o), [rg(in0), rg(in1)], [rg(out)])
+
+    def fill(out, value):
+        op("V", lambda: v.memset(ap(out), value), [], [rg(out)])
 
     def cp(q, out, in_):
         if q == "V":
@@ -171,7 +194,8 @@ def rank_program(g, core, T, topo):
 
     def both(out, win, tab, k):
         st = out[3] if len(out) == 4 else 1
-        gather("V", (out[0], out[1], out[1] + 16 * k * st - out[1] % st) + out[3:], win, (tab[0], tab[1], tab[1] + k))
+        if k > 0:
+            gather("V", (out[0], out[1], out[1] + 16 * k * st - out[1] % st) + out[3:], win, (tab[0], tab[1], tab[1] + k))
         if k < 20:
             gather("S", (out[0], out[1] + 16 * k * st, out[2]) + out[3:], win, (tab[0], tab[1] + k, tab[2]))
 
@@ -186,13 +210,8 @@ def rank_program(g, core, T, topo):
     def held(sc="SC"):
         return (sc, 15, C, 16)
 
-    def sample(out, sc="SC"):
-        ts(out, held(sc), K, 160.25, A.mult, A.add)
-
-    def table(out, w, k):
-        scan((w[0], w[1], w[1] + 16 * k))
-        scan((w[0], w[1] + 16 * k, w[2]))
-        sample(out)
+    def sample(out, sc="SC", zero=160.25):
+        ts(out, held(sc), K, zero, A.mult, A.add)
 
     def choose(out, bits, pairs):
         op("V", lambda: v.tensor_tensor_scan(ap(out), ap(bits), ap(pairs), 0.0, A.mult, A.add), [rg(bits), rg(pairs)], [rg(out)])
@@ -203,14 +222,14 @@ def rank_program(g, core, T, topo):
     def brg(b):
         return reg("PS", 512 * b, 512 * b + 512)
 
-    def evac(q, out, b, scale=None):
+    def evac(q, out, b, scale=None, lo=0):
         n = out[2] - out[1]
         if q == "V":
-            op("V", lambda: v.tensor_copy(ap(out), ap(bank(b, 0, n))), [brg(b)], [rg(out)])
+            op("V", lambda: v.tensor_copy(ap(out), ap(bank(b, lo, n))), [brg(b)], [rg(out)])
         elif scale is None:
-            op("S", lambda: s.activation(ap(out), ap(bank(b, 0, n)), COPY), [brg(b)], [rg(out)])
+            op("S", lambda: s.activation(ap(out), ap(bank(b, lo, n)), COPY), [brg(b)], [rg(out)])
         else:
-            op("S", lambda: s.activation(ap(out), ap(bank(b, 0, n)), COPY, scale=scale), [brg(b)], [rg(out)])
+            op("S", lambda: s.activation(ap(out), ap(bank(b, lo, n)), COPY, scale=scale), [brg(b)], [rg(out)])
 
     def mm(b, lq, ls, lo, rq, rs, start=True, stop=True, c0=0, c1=C):
         op("P", lambda: pe.matmul_mx(ap(bank(b, 0, c1 - c0)), T[lq][:, lo:lo + 128], T[ls][:, lo:lo + 128], T[rq][:, c0:c1], T[rs][:, c0:c1], start, stop),
@@ -230,16 +249,13 @@ def rank_program(g, core, T, topo):
 
     IOS = al("IOS")
     PM, PF, K = ("PC", 0, 1), ("PC", 1, 2), ("PC", 2, 3)
-
-    def own(r):
-        return ("PL", 40 * r + 1, 40 * r + 40, 2)
-
-    def send_list(r):
-        send(T.cores[rank ^ MASK[r]], T["LL%d" % r][:, 0:40], T.PL[:, 40 * r:40 * r + 40], [reg("PL", 40 * r, 40 * r + 40)], reg("LL%d" % r, 0, 40), "al%d" % r)
+    J, JH, JJ = part("J", 0), part("J", 1), part("J", 2)
+    KP, KN = part("KS", 0), part("KS", 1)
+    DL = part("DL", 0)
 
     def offsets4(r, which):
         for t in which:
-            ts(("F4%d" % r, 20 * t, 20 * t + 20), own(r), 4.0, t - 0.75, A.mult, A.add)
+            ts(part("F4%d" % r, t), part("OL", r), 4.0, t + 0.25, A.mult, A.add)
 
     dma("Y", T.FLI[:], T.fl[:], [], [reg("FLI")])
     dma("S", T.UT[:], T.u[:], [], [reg("UT")])
@@ -250,8 +266,10 @@ def rank_program(g, core, T, topo):
     op("G", lambda: g.iota(T.CI[:], [[16, 20]], 0, 0), [], [reg("CI")])
     op("G", lambda: g.iota(ap(IOS), [[1, C]], -160, 0, allow_small_or_imprecise_dtypes=True), [], [rg(IOS)])
     send(T.cores[rank ^ MASK[0]], T.LI[:], T.FLI[:], [reg("FLI")], reg("LI"), "al0")
-    for name in ("PL", "PK", "ET"):
-        op("V", lambda: v.memset(T[name][:], 0.0), [], [reg(name)])
+    for name in ("BB", "ET", "FAR"):
+        fill(al(name), 0.0)
+    fill(("KS", 40, 50), 4.0)
+    fill(("KS", 50, 60), 1.0)
     ts(al("QA"), al("Q16"), 15, None, A.bitwise_and)
     ts(PF, ("Q16", 0, 1), -288.0, None, A.add)
     cp("V", al("UO"), ("CI", 0, 8))
@@ -260,151 +278,203 @@ def rank_program(g, core, T, topo):
     ts(("CA", 16, 32), al("QA"), 0.0, None, A.not_equal)
     ts(al("PT"), al("CI"), 0.0, PM, A.mult, A.add)
     tt(al("C16"), ("CA", 0, 16), ("CA", 16, 32), A.max)
-    cp("S", ("FW", C, 2 * C), IOS)
     gather("S", al("CSC"), al("C16"), al("PT"))
+    for lo, hi, scale, bias, at in ((0, 96, 1.0, -96.0, 0), (96, 192, 1.0, 224.0, 416), (192, C, 2.0, 192.0, 512)):
+        out = ("WK", C + lo, C + hi)
+        op("S", lambda: s.activation(ap(out), T.IOS[:, lo:hi], F_.Identity, bias=bias, scale=scale), [rg(IOS)], [rg(out)])
+        for t in range(int(scale)):
+            cp("S", ("FW", at + t, at + int(scale) * (hi - lo), int(scale)), ("IOS", lo, hi))
     ts(K, ("QA", 0, 1), 15.0, 1.0 / BIG, A.is_equal, A.max)
     ts(("ET", 3, 515, 4), ("IOS", 0, 128), PF, 0.5, A.is_equal, A.mult)
-    ts(al("J"), al("CI"), PM, 0.25, A.add, A.add)
+    ts(J, al("CI"), PM, None, A.add)
+    fill(odd(al("FAR")), 640.0)
 
     def eq(b):
         quant("EQ", "ES", "ET", 128 * b, 128 * b + 128, 3 - b)
     eq(0)
+    ts(KP, part("KS", 2), K, K, A.mult, A.mult)
     eq(1)
+    ts(JH, J, 0.5, None, A.add)
+    ts(JJ, J, 2.0, 0.5, A.mult, A.add)
+    ts(KN, KP, -1.0, None, A.mult)
+    cp("V", al("FT0"), al("FLI"))
     quant("UQ", "US", "UT")
     eq(2)
     op("S", lambda: s.activation(T.US2[:], T.US[:].indirect(T.UO[:]), COPY), [reg("US"), reg("UO")], [reg("US2")])
     op("V", lambda: v.tensor_copy(u32(T.UQ2[:]), u32(T.UQ[:]).indirect(T.UO[:])), [reg("UQ"), reg("UO")], [reg("UQ2")])
-    ts(own(0), al("FLI"), 0.25, None, A.add)
+    gather("S", al("FS0"), IOS, al("FT0"))
+    cp("V", part("OL", 0), al("FLI"))
     quant("QX0", "SX0", "X0", *CUT[0])
     offsets4(0, (3, 2))
     quant("QX0", "SX0", "X0", *CUT[1])
-    for r in range(3):
-        op("S", lambda: s.activation(T["LL%d" % r][:, 41:80:2], T.J[:], F_.Identity, bias=320.0), [reg("J")], [rg(("LL%d" % r, 41, 80, 2))])
 
     for r, m in enumerate(MASK):
         dst = T.cores[rank ^ m]
         n_ = lambda k: k + str(r)
-        X, QX, SX, FS, FI, F4, B3, LP, LL, LQ, LS = [n_(k) for k in ("X", "QX", "SX", "FS", "FI", "F4", "B3", "LP", "LL", "LQ", "LS")]
-        XF, QF, SF, F, M, Z, QZ, SZ, PW, WN, TB, AS, AT, RI, RT = [n_(k) for k in ("XF", "QF", "SF", "F", "M", "Z", "QZ", "SZ", "PW", "WN", "TB", "AS", "AT", "RI", "RT")]
+        X, QX, SX, FS, F4, B3, LP, LQ, LS = [n_(k) for k in ("X", "QX", "SX", "FS", "F4", "B3", "LP", "LQ", "LS")]
+        XF, QF, SF, F, M, Z, QZ, SZ, PW, WN, TB, AS, AT = [n_(k) for k in ("XF", "QF", "SF", "F", "M", "Z", "QZ", "SZ", "PW", "WN", "TB", "AS", "AT")]
         nxt = str(r + 1)
+        OL, pairs, plus, minus = part("OL", r), part("PP", r, 40), part("BB", 2 * r, 40), part("BB", 2 * r + 1, 40)
 
         for i, (lo, hi) in enumerate(CUT):
             mm(4 + i, "UQ2", "US2", 0, QX, SX, c0=lo, c1=hi)
+        send(dst, T[LS][:], T[SX][:], [reg(SX)], reg(LS), n_("asc"))
         if r > 0:
             for b in range(4):
                 mm(b, "EQ", "ES", 128 * b, QX, SX)
-        gather("S", lane(XF, 3), al(X), (F4, 60, 80))
-        offsets4(r, (1, 0))
-        op("V", lambda: v.tensor_scalar(T.SG[:, 0:H], ap(bank(4, 0, H)), 0.0, None, A.is_gt), [brg(4)], [reg("SG", 0, H)])
+            if r > 1:
+                scan(al(FS), "SC2")
+            else:
+                gather("S", lane(XF, 3), al(X), part(F4, 3))
+                offsets4(r, (2, 1))
+        else:
+            gather("S", lane(XF, 3), al(X), part(F4, 3))
+            offsets4(r, (1, 0))
+        op("V", lambda: v.tensor_scalar(T.SG[:, 0:H], ap(bank(4, 0, H)), 0.0, 0.5, A.is_gt, A.subtract), [brg(4)], [reg("SG", 0, H)])
         op("S", lambda: s.activation(T.SG[:, H:C], ap(bank(5, 0, H)), F_.Sign, bias=-2.0 ** -93), [brg(5)], [reg("SG", H, C)])
-        for lo, hi in CUT:
-            scan(("SG", lo, hi))
-        bits = ("PK", 40 * r, 40 * r + 40)
-        mine = ("PK", 40 * r + 1, 40 * r + 40, 2)
-        ts(mine, held(), K, 0.5, A.mult, A.is_gt)
-        send(dst, T[LP][:], ap(bits), [rg(bits)], reg(LP), n_("apk"))
-        send(dst, T[LS][:], T[SX][:], [reg(SX)], reg(LS), n_("asc"))
+        if r > 1:
+            ts(OL, held("SC2"), K, 160.0, A.mult, A.add)
+        scan(("SG",) + CUT[0], "SCS")
+        if r > 0:
+            tt(DL, OL, J, A.subtract)
+            tt(odd(pairs), OL, JH, A.add)
+        scan(("SG",) + CUT[1], "SCS")
+        if r > 0:
+            offsets4(r, (3,) if r > 1 else (0,))
+            tt(even(pairs), held("SCS"), DL, A.mult)
+            send(dst, T[LP][:], ap(pairs), [rg(pairs)], reg(LP), n_("apk"))
+        else:
+            tt(odd(plus), held("SCS"), KP, A.mult)
+            send(dst, T[LP][:], ap(plus), [rg(plus)], reg(LP), n_("apk"))
         send(dst, u8(T[LQ][:]), u8(T[QX][:]), [reg(QX)], reg(LQ), n_("aq"))
+
         if r == 0:
             eq(3)
-            cp("V", al("FT0"), al("FLI"))
             for b in range(4):
                 mm(b, "EQ", "ES", 128 * b, QX, SX)
             dma("Y", u8(T.WQ[:]), T.wc[:], [reg(LQ)], [reg("WQ")])
             dma("Y", T.WS[:], T.ws[:], [], [reg("WS")])
             dma("Y", T.VT[:], T.v[:], [], [reg("VT")])
+            for t in (2, 1):
+                gather("S", lane(XF, t), al(X), part(F4, t))
+            gather("V", lane(XF, 0), al(X), part(F4, 0))
+            tt(DL, al("LI"), J, A.subtract)
+            tt(odd(pairs), al("LI"), JH, A.add)
+            tt(even(pairs), held("SCS"), DL, A.mult)
+            sides = ((al(LP), pairs),)
+        else:
+            if r > 1:
+                offsets4(r, (2, 1, 0))
+                gather("S", lane(XF, 3), al(X), part(F4, 3))
+            gather("V" if r > 1 else "S", lane(XF, 1), al(X), part(F4, 1))
+            gather("S", lane(XF, 2), al(X), part(F4, 2))
+            gather("V", lane(XF, 0), al(X), part(F4, 0))
+            tt(odd(plus), held("SCS"), KP, A.mult)
+            tt(odd(minus), held("SCS"), KN, A.mult)
+            sides = ((plus, al(LP)), (minus, al(LP)))
 
-        for t in (2, 1):
-            gather("S", lane(XF, t), al(X), (F4, 20 * t, 20 * t + 20))
-        gather("V", lane(XF, 0), al(X), (F4, 0, 20))
-        if r == 0:
-            ts((LL, 1, 40, 2), al("LI"), 0.25, None, A.add)
-        ts(al("SN"), mine, -2.0, 1.0, A.mult, A.add)
-        tt((LL, 0, 40, 2), al("J"), (LL, 1, 40, 2), A.subtract)
-        tt((LL, 40, 80, 2), (LL, 1, 40, 2), (LL, 41, 80, 2), A.subtract)
-        for lo in (0, 40):
-            choose(("AB", lo, lo + 40), bits, (LL, lo, lo + 40))
-        for lo in (0, 40):
-            tt(("AB", lo, lo + 40, 2), (LL, lo, lo + 40, 2), al("SN"), A.mult)
-        for b in range(3):
+        def meet_in_psum():
+            for b in range(4):
+                mm(4 + b, "EQ", "ES", 128 * b, QF, SF, True, False)
+            for b in range(4):
+                mm(4 + b, "EQ", "ES", 128 * b, LQ, LS, False, True)
+        pack = [lambda: quant(QF, SF, XF, *CUT[0]), lambda: (quant(QF, SF, XF, *CUT[1]), meet_in_psum())]
+        for _ in range(2 - QGAP):
+            pack.pop(0)()
+        for b in range(FEV):
             evac("S", plane(F, b), b)
-        if r == 0:
-            gather("S", al("FS0"), IOS, al("FT0"))
 
         def tb(i):
-            return (TB, 20 * i, 20 * i + 20)
-        for i in range(2):
-            choose(("TF", 40 * i, 40 * i + 40), al(LP), ("AB", 40 * i, 40 * i + 40))
-        for i in range(2):
-            cp("V", tb(i), ("TF", 40 * i + 1, 40 * i + 40, 2))
+            return part(TB, i)
+        t0, t1, t2 = [part("TF", i, 40) for i in range(3)]
+
+        def read(q, name, b, bk):
+            return [lambda i=i: evac(q, (name, C * b + i, C * b + i + PIECE), bk, None, i) for i in range(0, C, PIECE)]
+        early = {"V": pack + [lambda: tt(even(t1), odd(t0), JJ, A.not_equal), lambda: choose(t2, al("FAR"), t1), lambda: ts(tb(1), odd(t2), 0.5, None, A.mult)],
+                 "S": [x for b in range(FEV, 3) for x in read("S", F, b, b)]}
+        if r == 0:
+            early["V"] = [lambda: tt(DL, odd(pairs), odd(t0), A.subtract), lambda: tt(odd(t1), DL, odd(pairs), A.add)] + early["V"]
+        if r == 1:
+            early["V"] += [lambda: quant("VQ", "VS", "VT")]
+
+        def mp(q, x):
+            return lambda: evac(q, (M, C * x[0] + x[1], C * x[0] + x[2]), 4 + x[0], None, x[1])
+        late = {"V": [mp("V", x) for x in MV], "S": [mp("S", x) for x in MS]}
+
+        def wait(k):
+            for q in "VS":
+                if len(late[q]) > NW - k + (q == "V"):
+                    late[q].pop(0)()
+                elif early[q]:
+                    early[q].pop(0)()
+        choose(t0, *sides[0])
+        if r > 0:
+            choose(t1, *sides[1])
+        ts(tb(0), odd(t0), 0.5, None, A.mult)
         w = (WN, 0, C)
         both(w, IOS, tb(0), 10)
-        quant(QF, SF, XF, *CUT[0])
         cur, pt, pw = 0, 1, 1
         for k, step in enumerate(STEPS):
-            w2 = ("FW", 0, C) if k == len(STEPS) - 1 else (WN, C * k + C, C * k + 2 * C)
+            wait(k)
+            w2 = ("WK", 0, C) if k == len(STEPS) - 1 else (WN, C * k + C, C * k + 2 * C)
             if step == "g":
                 both(w2, w, tb(cur), 10)
                 w, pw = w2, pw + pt
             else:
-                scan(w)
-                if step == "tg":
-                    both(w2, w, tb(cur), 4)
+                sc = ("SC", "SC3")[k % 2]
+                scan(w, sc)
+                both(w2, w, tb(cur), TGV[max(cur - 1, 0)])
                 cur = max(cur + 1, 2)
-                sample(tb(cur))
-                if step == "tg":
-                    w, pt, pw = w2, pw, pw + pt
-                else:
-                    pt = pw
-                    for b in range(2):
-                        evac("S", plane(M, b), 4 + b)
-            if k == 0:
-                quant(QF, SF, XF, *CUT[1])
-                for b in range(4):
-                    mm(4 + b, "EQ", "ES", 128 * b, QF, SF, True, False)
-                for b in range(4):
-                    mm(4 + b, "EQ", "ES", 128 * b, LQ, LS, False, True)
-        assert pw >= C - 1
-        both(al(AS), al("FW"), tb(1), 10)
+                sample(tb(cur), sc)
+                w, pt, pw = w2, pw, pw + pt
+        assert 3 * pw >= C - 1 and not early["V"] and not early["S"]
+        wait(NW - 2)
+        scan(w)
+        both(al("AW"), al("WK"), tb(1), TGV[-2])
+        sample(tb(cur + 1))
+        wait(NW - 1)
+        scan(al("AW"), "SC3")
+        both(("FW", 96, 96 + C), w, tb(cur + 1), TGV[-1])
+        sample(tb(cur + 2), "SC3", 256.25)
+        wait(NW)
+        both(al(AS), al("FW"), tb(cur + 2), 10)
+        late["V"].pop(0)()
         scan(al(AS))
+        for x in MEND:
+            mp("S", x)()
+        assert not late["V"] and not late["S"]
         sample(al(AT))
-        for b in range(2, 4):
-            evac("S", plane(M, b), 4 + b)
 
-        fi = al(FI)
-        if r < 2:
+        fi = part("FI", r + 1)
+        if r == 0:
             def piece(q, lo, hi):
                 gather(q, (Z, 64 * lo + 3, 64 * hi, 4), plane(M, 3), (AT, lo, hi))
-            both(al("FS" + nxt), al(FS), al(AT), 10)
+            both(al("FS1"), al(FS), al(AT), 10)
             piece("V", 0, 4)
             for b in range(3):
                 gather("S", lane(Z, b), plane(M, b), al(AT))
-            scan(al("FS" + nxt), "SC2")
+            scan(al("FS1"), "SC2")
             piece("V", 4, 8)
-            sample(al(RT), "SC2")
+            sample(al("FT0"), "SC2")
             piece("V", 8, 12)
             piece("S", 12, 20)
-            scatter(al(RI), al(RT), 0, AHEAD)
-            op("S", lambda: s.activation(ap(own(r + 1)), ap(held("SC2")), F_.Identity, bias=160.25, scale=ap(K)), [rg(held("SC2")), rg(K)], [rg(own(r + 1))])
-            send_list(r + 1)
+            scatter(al("RI"), al("FT0"), 0, AHEAD)
         else:
             scatter(al("AI"), al(AT))
             for b in range(3):
                 gather("S", lane(Z, b), plane(M, b), al(AT))
-            gather("V", lane(Z, 3), plane(M, 3), al(AT))
-            gather("S", al(RI), al("AI"), al("FI%d" % (r - 1)))
+            both(lane(Z, 3), plane(M, 3), al(AT), ZV)
+            gather("S", al("RI"), al("AI"), part("FI", r))
         for lo, hi in CUT:
             quant(QZ, SZ, Z, lo, hi)
-        if r < 2:
-            scatter(al(RI), al(RT), AHEAD, 20)
-        if r == 1:
-            quant("VQ", "VS", "VT")
-        scan(al(RI))
-        if r < 2:
-            offsets4(r + 1, (3,))
+        if r == 0:
+            scatter(al("RI"), al("FT0"), AHEAD, 20)
+        scan(al("RI"))
+        if r == 0:
+            ts(part("OL", 1), held("SC2"), K, 160.0, A.mult, A.add)
         sample(fi)
-        if r < 2:
-            offsets4(r + 1, (2,))
+        if r == 0:
+            offsets4(1, (3,))
         mm(0, "WQ", "WS", 0, QZ, SZ, c0=0, c1=H)
         mm(4, "WQ", "WS", 0, QZ, SZ, c0=H, c1=C)
         for b in (1, 3, 2):
@@ -414,6 +484,11 @@ def rank_program(g, core, T, topo):
         for b in (1, 3, 2):
             evac("S", plane(PW, b), 4 + b, 0.015625)
         gather("S", al(B3), plane(PW, 3), fi)
+        if r == 1:
+            gather("S", al("FS" + nxt), al(FS), al(AT))
+        if r == 2:
+            op("S", lambda: s.activation(T.LNF[:], T[FS][:].indirect(T[AT][:]), F_.Identity, bias=160.0), [reg(FS), reg(AT)], [reg("LNF")])
+            dma("S", T.ln[:], T.LNF[0:128:16, :], [reg("LNF")], [], "out")
         for b in range(3):
             op("V", lambda: v.tensor_tensor(ap(lane("X" + nxt, b)), ap(plane(PW, b)).indirect(ap(fi)), ap(plane(F, b)), A.add),
                [rg(plane(PW, b)), rg(fi), rg(plane(F, b))], [rg(lane("X" + nxt, b))])
@@ -422,9 +497,6 @@ def rank_program(g, core, T, topo):
             op("V", lambda: v.tensor_tensor(ap(out), T[B3][:, lo:hi], ap(bank(3, lo, hi - lo)), A.add), [reg(B3), brg(3)], [rg(out)])
         for lo, hi in CUT:
             quant("QX" + nxt, "SX" + nxt, "X" + nxt, lo, hi)
-        if r == 2:
-            op("S", lambda: s.activation(T.LNF[:], T[FS][:].indirect(T[AT][:]), F_.Identity, bias=160.0), [reg(FS), reg(AT)], [reg("LNF")])
-            dma("S", T.ln[:], T.LNF[0:128:16, :], [reg("LNF")], [], "out")
 
     for i, (lo, hi) in enumerate(CUT):
         mm(4 + i, "VQ", "VS", 0, "QX3", "SX3", c0=lo, c1=hi)

from concourse.mybir import dt, AluOpType, ActivationFunctionType

C = 320
H = C // 2
CUT = ((0, H), (H, C))
MASK = [1, 2, 4]
STEPS = "g tg g tg g tg tg g tg g".split()
NW = len(STEPS) + 2
BIG = 2.0 ** 40
PIECE = 80
ZV = 18
TGV = (4, 4, 4, 4, 4, 4, 4)
FEV = 3
QGAP = 0
MV = [(0, 0, 80), (0, 80, 160), (0, 160, 240), (0, 240, 320), (3, 0, 80), (3, 80, 160)]
MS = [(1, 0, 80), (1, 80, 160), (1, 160, 240), (1, 240, 320)]
MEND = [(2, 0, 320), (3, 160, 320)]
AHEAD = 18

SCRATCH = {
    "Q16": ("sbuf", [128, 16], "int32"), "QA": ("sbuf", [128, 16], "int32"), "CI": ("sbuf", [128, 20], "int32"),
    "PC": ("sbuf", [128, 8], "float32"), "CA": ("sbuf", [128, 32], "float32"), "C16": ("sbuf", [128, 16], "bfloat16"),
    "PT": ("sbuf", [128, 20], "uint16"), "UO": ("sbuf", [128, 8], "uint16"),
    "CSC": ("sbuf", [128, C], "bfloat16"), "J": ("sbuf", [128, 60], "float32"), "KS": ("sbuf", [128, 60], "float32"),
    "FAR": ("sbuf", [128, 40], "float32"),
    "IOS": ("sbuf", [128, C], "bfloat16"), "FW": ("sbuf", [128, 768], "bfloat16"),
    "WK": ("sbuf", [128, 2 * C], "bfloat16"), "AW": ("sbuf", [128, C], "bfloat16"),
    "ET": ("sbuf", [128, 520], "bfloat16"),
    "EQ": ("sbuf", [128, 512], "float8_e4m3fn_x4"), "ES": ("sbuf", [128, 512], "uint8"),
    "UT": ("sbuf", [128, 512], "bfloat16"), "VT": ("sbuf", [128, 512], "bfloat16"),
    "UQ": ("sbuf", [128, 128], "float8_e4m3fn_x4"), "US": ("sbuf", [128, 128], "uint8"),
    "UQ2": ("sbuf", [128, 128], "float8_e4m3fn_x4"), "US2": ("sbuf", [128, 128], "uint8"),
    "VQ": ("sbuf", [128, 128], "float8_e4m3fn_x4"), "VS": ("sbuf", [128, 128], "uint8"),
    "WQ": ("sbuf", [128, 512], "float8_e4m3fn_x4"), "WS": ("sbuf", [128, 512], "uint8"),
    "FLI": ("sbuf", [128, 20], "int32"), "LI": ("sbuf", [128, 20], "int32"), "FT0": ("sbuf", [128, 20], "uint16"),
    "OL": ("sbuf", [128, 60], "float32"), "DL": ("sbuf", [128, 40], "float32"),
    "PP": ("sbuf", [128, 160], "float32"), "BB": ("sbuf", [128, 240], "bfloat16"), "TF": ("sbuf", [128, 120], "float32"),
    "SG": ("sbuf", [128, C], "bfloat16"), "SC": ("sbuf", [128, C], "bfloat16"), "SC2": ("sbuf", [128, C], "bfloat16"), "SC3": ("sbuf", [128, C], "bfloat16"), "SCS": ("sbuf", [128, C], "bfloat16"),
    "AI": ("sbuf", [128, C], "bfloat16"), "RI": ("sbuf", [128, C], "bfloat16"), "FI": ("sbuf", [128, 80], "uint16"),
    "LP0": ("sbuf", [128, 40], "bfloat16"), "LP1": ("sbuf", [128, 40], "float32"), "LP2": ("sbuf", [128, 40], "float32"),
    "LNF": ("sbuf", [128, C], "float32"), "YS": ("sbuf", [128, C], "float32"),
    "QX3": ("sbuf", [128, C], "float8_e4m3fn_x4"), "SX3": ("sbuf", [128, C], "uint8"), "X3": ("sbuf", [128, 4 * C], "bfloat16"),
    "PS": ("psum", [128, 4096], "float32"),
}
for _r in range(3):
    SCRATCH.update({
        "X%d" % _r: ("sbuf", [128, 4 * C], "bfloat16"),
        "QX%d" % _r: ("sbuf", [128, C], "float8_e4m3fn_x4"), "SX%d" % _r: ("sbuf", [128, C], "uint8"),
        "FS%d" % _r: ("sbuf", [128, C], "bfloat16"),
        "F4%d" % _r: ("sbuf", [128, 80], "uint16"), "B3%d" % _r: ("sbuf", [128, C], "float32"),
        "LQ%d" % _r: ("sbuf", [128, C], "float8_e4m3fn_x4"), "LS%d" % _r: ("sbuf", [128, C], "uint8"),
        "XF%d" % _r: ("sbuf", [128, 4 * C], "bfloat16"),
        "QF%d" % _r: ("sbuf", [128, C], "float8_e4m3fn_x4"), "SF%d" % _r: ("sbuf", [128, C], "uint8"),
        "F%d" % _r: ("sbuf", [128, 3 * C], "bfloat16"), "M%d" % _r: ("sbuf", [128, 4 * C], "bfloat16"),
        "Z%d" % _r: ("sbuf", [128, 4 * C], "bfloat16"),
        "QZ%d" % _r: ("sbuf", [128, C], "float8_e4m3fn_x4"), "SZ%d" % _r: ("sbuf", [128, C], "uint8"),
        "PW%d" % _r: ("sbuf", [128, 4 * C], "float32"),
        "WN%d" % _r: ("sbuf", [128, C * NW], "bfloat16"), "AS%d" % _r: ("sbuf", [128, C], "bfloat16"),
        "TB%d" % _r: ("sbuf", [128, 20 * 10], "uint16"), "AT%d" % _r: ("sbuf", [128, 20], "uint16"),
    })
SEMAPHORES = ["sV", "sS", "sP", "sG", "lsent", "out", "al0"] + ["d%d" % i for i in range(7)] + [k + str(r) for r in range(3) for k in ("apk", "aq", "asc")]


def rank_program(g, core, T, topo):
    rank = T.rank_of(core)
    if rank is None:
        return
    A = AluOpType
    F_ = ActivationFunctionType
    COPY = F_.Copy
    v, s, pe = g.vector, g.scalar, g.tensor
    queue = {"V": v, "S": s, "P": pe, "G": g, "Y": g.sync}

    count = {}
    known = {q: {} for q in queue}
    behind = {}
    writers, readers = {}, {}

    def reg(name, lo=0, hi=None, lane=None):
        return (name, lo, T[name].shape[1] if hi is None else hi, lane)

    def meet(a, b):
        return a[1] < b[2] and b[1] < a[2] and (a[3] is None or b[3] is None or a[3] == b[3])

    def need(q, toks):
        best = {}
        for (sem, val) in toks:
            if known[q].get(sem, 0) < val and best.get(sem, 0) < val:
                best[sem] = val
        for sem in list(best):
            for sem2, val2 in best.items():
                if sem2 != sem and behind.get((sem2, val2), {}).get(sem, 0) >= best[sem]:
                    best[sem] = 0
                    break
        for sem, val in best.items():
            if val:
                queue[q].wait_ge(T.sem[sem], val)
                known[q][sem] = max(val, known[q].get(sem, 0))
                for k2, v2 in behind.get((sem, val), {}).items():
                    known[q][k2] = max(v2, known[q].get(k2, 0))

    def deps(q, rd, wr, dma):
        toks = []
        for r_ in rd:
            toks += [t for (x, t, e) in writers.get(r_[0], []) if meet(x, r_)]
            if r_[0] == "PS":
                toks += [t for (x, t, e) in readers.get("PS", []) if meet(x, r_) and e != q]
        for w_ in wr:
            toks += [t for (x, t, e) in writers.get(w_[0], []) if meet(x, w_) and not (q == "P" and e == q)]
            toks += [t for (x, t, e) in readers.get(w_[0], []) if meet(x, w_) and not (q == "P" and e == q)]
        need(q, toks)

    def note(q, rd, wr, tok, e):
        behind[tok] = dict(known[q])
        for r_ in rd:
            readers.setdefault(r_[0], []).append((r_, tok, e))
        for w_ in wr:
            writers.setdefault(w_[0], []).append((w_, tok, e))

    def op(q, call, rd, wr):
        deps(q, rd, wr, False)
        sem = "s" + q
        count[sem] = count.get(sem, 0) + 1
        call().then_inc(T.sem[sem], 1)
        note(q, rd, wr, (sem, count[sem]), q)

    ndma = [0]

    def dma(q, out, in_, rd, wr, sem=None):
        deps(q, rd, wr, True)
        if sem is None:
            sem = "d%d" % ndma[0]
            ndma[0] += 1
        count[sem] = count.get(sem, 0) + 16
        queue[q].dma_start(out, in_).then_inc(T.sem[sem], 16)
        note(q, rd, wr, (sem, 16), "dma" + sem)

    def send(dst, out, in_, rd, land, sem):
        deps("G", rd, [], True)
        rid, pid = topo.addr(dst, core)
        g.remote_dma(out, in_, T.sem[sem], T.sem["lsent"], pid, rid, topo.mask(core, dst))
        count["lsent"] = count.get("lsent", 0) + len(topo.engines(core, dst))
        count[sem] = len(topo.engines(dst, core))
        behind[(sem, count[sem])] = {}
        writers.setdefault(land[0], []).append((land, (sem, count[sem]), "far"))

    def u8(ap):
        return ap.bitcast(dt.uint8)

    def u32(ap):
        return ap.bitcast(dt.uint32)

    def ap(p):
        return T[p[0]][:, p[1]:p[2]] if len(p) == 3 else T[p[0]][:, p[1]:p[2]:p[3]]

    def rg(p):
        return reg(p[0], p[1], p[2]) if len(p) == 3 else reg(p[0], p[1] - p[1] % p[3], p[2], p[1] % p[3])

    def al(name):
        return (name, 0, T[name].shape[1])

    def part(name, i, n=20):
        return (name, n * i, n * i + n)

    def even(p):
        return (p[0], p[1], p[2], 2)

    def odd(p):
        return (p[0], p[1] + 1, p[2], 2)

    def ts(out, in0, s1, s2, op0, op1=None):
        col = [x for x in (s1, s2) if isinstance(x, tuple)]
        a1, a2 = [ap(x) if isinstance(x, tuple) else x for x in (s1, s2)]
        more = [] if op1 is None else [op1]
        op("V", lambda: v.tensor_scalar(ap(out), ap(in0), a1, a2, op0, *more), [rg(x) for x in [in0] + col], [rg(out)])

    def tt(out, in0, in1, o):
        op("V", lambda: v.tensor_tensor(ap(out), ap(in0), ap(in1), o), [rg(in0), rg(in1)], [rg(out)])

    def fill(out, value):
        op("V", lambda: v.memset(ap(out), value), [], [rg(out)])

    def cp(q, out, in_):
        if q == "V":
            op("V", lambda: v.tensor_copy(ap(out), ap(in_)), [rg(in_)], [rg(out)])
        else:
            op("S", lambda: s.activation(ap(out), ap(in_), COPY), [rg(in_)], [rg(out)])

    def gather(q, out, win, tab):
        if q == "V":
            op("V", lambda: v.tensor_copy(ap(out), ap(win).indirect(ap(tab))), [rg(win), rg(tab)], [rg(out)])
        else:
            op("S", lambda: s.activation(ap(out), ap(win).indirect(ap(tab)), COPY), [rg(win), rg(tab)], [rg(out)])

    def both(out, win, tab, k):
        st = out[3] if len(out) == 4 else 1
        if k > 0:
            gather("V", (out[0], out[1], out[1] + 16 * k * st - out[1] % st) + out[3:], win, (tab[0], tab[1], tab[1] + k))
        if k < 20:
            gather("S", (out[0], out[1] + 16 * k * st, out[2]) + out[3:], win, (tab[0], tab[1] + k, tab[2]))

    def scatter(out, tab, lo=0, hi=20):
        op("V", lambda: v.tensor_copy(ap(out).indirect(T[tab[0]][:, lo:hi]), T.IOS[:, 16 * lo:16 * hi]), [rg(IOS), rg(tab)], [rg(out)])

    def scan(spread, sc="SC"):
        lo = spread[1] % C
        hi = lo + spread[2] - spread[1]
        op("V", lambda: v.tensor_tensor_scan(T[sc][:, lo:hi], T.CSC[:, lo:hi], ap(spread), 0.0, A.mult, A.add), [rg(spread), reg("CSC")], [reg(sc, lo, hi)])

    def held(sc="SC"):
        return (sc, 15, C, 16)

    def sample(out, sc="SC", zero=160.25):
        ts(out, held(sc), K, zero, A.mult, A.add)

    def choose(out, bits, pairs):
        op("V", lambda: v.tensor_tensor_scan(ap(out), ap(bits), ap(pairs), 0.0, A.mult, A.add), [rg(bits), rg(pairs)], [rg(out)])

    def bank(b, lo=0, n=C):
        return ("PS", 512 * b + lo, 512 * b + lo + n)

    def brg(b):
        return reg("PS", 512 * b, 512 * b + 512)

    def evac(q, out, b, scale=None, lo=0):
        n = out[2] - out[1]
        if q == "V":
            op("V", lambda: v.tensor_copy(ap(out), ap(bank(b, lo, n))), [brg(b)], [rg(out)])
        elif scale is None:
            op("S", lambda: s.activation(ap(out), ap(bank(b, lo, n)), COPY), [brg(b)], [rg(out)])
        else:
            op("S", lambda: s.activation(ap(out), ap(bank(b, lo, n)), COPY, scale=scale), [brg(b)], [rg(out)])

    def mm(b, lq, ls, lo, rq, rs, start=True, stop=True, c0=0, c1=C):
        op("P", lambda: pe.matmul_mx(ap(bank(b, 0, c1 - c0)), T[lq][:, lo:lo + 128], T[ls][:, lo:lo + 128], T[rq][:, c0:c1], T[rs][:, c0:c1], start, stop),
           [reg(lq, lo, lo + 128), reg(ls, lo, lo + 128), reg(rq, c0, c1), reg(rs, c0, c1)], [brg(b)])

    def quant(q, sc, t, c0=0, c1=None, at=None):
        c1 = T[q].shape[1] if c1 is None else c1
        at = 4 * c0 if at is None else at
        op("V", lambda: v.quantize_mx(T[q][:, c0:c1], T[sc][:, c0:c1], T[t][:, at:at + 4 * (c1 - c0)]),
           [reg(t, at, at + 4 * (c1 - c0))], [reg(q, c0, c1), reg(sc, c0, c1)])

    def plane(name, b):
        return (name, C * b, C * b + C)

    def lane(name, b):
        return (name, b, 4 * C, 4)

    IOS = al("IOS")
    PM, PF, K = ("PC", 0, 1), ("PC", 1, 2), ("PC", 2, 3)
    J, JH, JJ = part("J", 0), part("J", 1), part("J", 2)
    KP, KN = part("KS", 0), part("KS", 1)
    DL = part("DL", 0)

    def offsets4(r, which):
        for t in which:
            ts(part("F4%d" % r, t), part("OL", r), 4.0, t + 0.25, A.mult, A.add)

    dma("Y", T.FLI[:], T.fl[:], [], [reg("FLI")])
    dma("S", T.UT[:], T.u[:], [], [reg("UT")])
    for q, (lo, hi) in zip("YS", CUT):
        dma(q, T.X0[:, 4 * lo:4 * hi], T.x[:, 4 * lo:4 * hi], [], [reg("X0", 4 * lo, 4 * hi)])

    op("G", lambda: g.iota(T.Q16[:], [[-1, 16]], 128, 1), [], [reg("Q16")])
    op("G", lambda: g.iota(T.CI[:], [[16, 20]], 0, 0), [], [reg("CI")])
    op("G", lambda: g.iota(ap(IOS), [[1, C]], -160, 0, allow_small_or_imprecise_dtypes=True), [], [rg(IOS)])
    send(T.cores[rank ^ MASK[0]], T.LI[:], T.FLI[:], [reg("FLI")], reg("LI"), "al0")
    for name in ("BB", "ET", "FAR"):
        fill(al(name), 0.0)
    fill(("KS", 40, 50), 4.0)
    fill(("KS", 50, 60), 1.0)
    ts(al("QA"), al("Q16"), 15, None, A.bitwise_and)
    ts(PF, ("Q16", 0, 1), -288.0, None, A.add)
    cp("V", al("UO"), ("CI", 0, 8))
    cp("V", PM, ("QA", 0, 1))
    ts(("CA", 0, 16), al("QA"), 15.0, BIG, A.is_equal, A.mult)
    ts(("CA", 16, 32), al("QA"), 0.0, None, A.not_equal)
    ts(al("PT"), al("CI"), 0.0, PM, A.mult, A.add)
    tt(al("C16"), ("CA", 0, 16), ("CA", 16, 32), A.max)
    gather("S", al("CSC"), al("C16"), al("PT"))
    for lo, hi, scale, bias, at in ((0, 96, 1.0, -96.0, 0), (96, 192, 1.0, 224.0, 416), (192, C, 2.0, 192.0, 512)):
        out = ("WK", C + lo, C + hi)
        op("S", lambda: s.activation(ap(out), T.IOS[:, lo:hi], F_.Identity, bias=bias, scale=scale), [rg(IOS)], [rg(out)])
        for t in range(int(scale)):
            cp("S", ("FW", at + t, at + int(scale) * (hi - lo), int(scale)), ("IOS", lo, hi))
    ts(K, ("QA", 0, 1), 15.0, 1.0 / BIG, A.is_equal, A.max)
    ts(("ET", 3, 515, 4), ("IOS", 0, 128), PF, 0.5, A.is_equal, A.mult)
    ts(J, al("CI"), PM, None, A.add)
    fill(odd(al("FAR")), 640.0)

    def eq(b):
        quant("EQ", "ES", "ET", 128 * b, 128 * b + 128, 3 - b)
    eq(0)
    ts(KP, part("KS", 2), K, K, A.mult, A.mult)
    eq(1)
    ts(JH, J, 0.5, None, A.add)
    ts(JJ, J, 2.0, 0.5, A.mult, A.add)
    ts(KN, KP, -1.0, None, A.mult)
    cp("V", al("FT0"), al("FLI"))
    quant("UQ", "US", "UT")
    eq(2)
    op("S", lambda: s.activation(T.US2[:], T.US[:].indirect(T.UO[:]), COPY), [reg("US"), reg("UO")], [reg("US2")])
    op("V", lambda: v.tensor_copy(u32(T.UQ2[:]), u32(T.UQ[:]).indirect(T.UO[:])), [reg("UQ"), reg("UO")], [reg("UQ2")])
    gather("S", al("FS0"), IOS, al("FT0"))
    cp("V", part("OL", 0), al("FLI"))
    quant("QX0", "SX0", "X0", *CUT[0])
    offsets4(0, (3, 2))
    quant("QX0", "SX0", "X0", *CUT[1])

    for r, m in enumerate(MASK):
        dst = T.cores[rank ^ m]
        n_ = lambda k: k + str(r)
        X, QX, SX, FS, F4, B3, LP, LQ, LS = [n_(k) for k in ("X", "QX", "SX", "FS", "F4", "B3", "LP", "LQ", "LS")]
        XF, QF, SF, F, M, Z, QZ, SZ, PW, WN, TB, AS, AT = [n_(k) for k in ("XF", "QF", "SF", "F", "M", "Z", "QZ", "SZ", "PW", "WN", "TB", "AS", "AT")]
        nxt = str(r + 1)
        OL, pairs, plus, minus = part("OL", r), part("PP", r, 40), part("BB", 2 * r, 40), part("BB", 2 * r + 1, 40)

        for i, (lo, hi) in enumerate(CUT):
            mm(4 + i, "UQ2", "US2", 0, QX, SX, c0=lo, c1=hi)
        send(dst, T[LS][:], T[SX][:], [reg(SX)], reg(LS), n_("asc"))
        if r > 0:
            for b in range(4):
                mm(b, "EQ", "ES", 128 * b, QX, SX)
            if r > 1:
                scan(al(FS), "SC2")
            else:
                gather("S", lane(XF, 3), al(X), part(F4, 3))
                offsets4(r, (2, 1))
        else:
            gather("S", lane(XF, 3), al(X), part(F4, 3))
            offsets4(r, (1, 0))
        op("V", lambda: v.tensor_scalar(T.SG[:, 0:H], ap(bank(4, 0, H)), 0.0, 0.5, A.is_gt, A.subtract), [brg(4)], [reg("SG", 0, H)])
        op("S", lambda: s.activation(T.SG[:, H:C], ap(bank(5, 0, H)), F_.Sign, bias=-2.0 ** -93), [brg(5)], [reg("SG", H, C)])
        if r > 1:
            ts(OL, held("SC2"), K, 160.0, A.mult, A.add)
        scan(("SG",) + CUT[0], "SCS")
        if r > 0:
            tt(DL, OL, J, A.subtract)
            tt(odd(pairs), OL, JH, A.add)
        scan(("SG",) + CUT[1], "SCS")
        if r > 0:
            offsets4(r, (3,) if r > 1 else (0,))
            tt(even(pairs), held("SCS"), DL, A.mult)
            send(dst, T[LP][:], ap(pairs), [rg(pairs)], reg(LP), n_("apk"))
        else:
            tt(odd(plus), held("SCS"), KP, A.mult)
            send(dst, T[LP][:], ap(plus), [rg(plus)], reg(LP), n_("apk"))
        send(dst, u8(T[LQ][:]), u8(T[QX][:]), [reg(QX)], reg(LQ), n_("aq"))

        if r == 0:
            eq(3)
            for b in range(4):
                mm(b, "EQ", "ES", 128 * b, QX, SX)
            dma("Y", u8(T.WQ[:]), T.wc[:], [reg(LQ)], [reg("WQ")])
            dma("Y", T.WS[:], T.ws[:], [], [reg("WS")])
            dma("Y", T.VT[:], T.v[:], [], [reg("VT")])
            for t in (2, 1):
                gather("S", lane(XF, t), al(X), part(F4, t))
            gather("V", lane(XF, 0), al(X), part(F4, 0))
            tt(DL, al("LI"), J, A.subtract)
            tt(odd(pairs), al("LI"), JH, A.add)
            tt(even(pairs), held("SCS"), DL, A.mult)
            sides = ((al(LP), pairs),)
        else:
            if r > 1:
                offsets4(r, (2, 1, 0))
                gather("S", lane(XF, 3), al(X), part(F4, 3))
            gather("V" if r > 1 else "S", lane(XF, 1), al(X), part(F4, 1))
            gather("S", lane(XF, 2), al(X), part(F4, 2))
            gather("V", lane(XF, 0), al(X), part(F4, 0))
            tt(odd(plus), held("SCS"), KP, A.mult)
            tt(odd(minus), held("SCS"), KN, A.mult)
            sides = ((plus, al(LP)), (minus, al(LP)))

        def meet_in_psum():
            for b in range(4):
                mm(4 + b, "EQ", "ES", 128 * b, QF, SF, True, False)
            for b in range(4):
                mm(4 + b, "EQ", "ES", 128 * b, LQ, LS, False, True)
        pack = [lambda: quant(QF, SF, XF, *CUT[0]), lambda: (quant(QF, SF, XF, *CUT[1]), meet_in_psum())]
        for _ in range(2 - QGAP):
            pack.pop(0)()
        for b in range(FEV):
            evac("S", plane(F, b), b)

        def tb(i):
            return part(TB, i)
        t0, t1, t2 = [part("TF", i, 40) for i in range(3)]

        def read(q, name, b, bk):
            return [lambda i=i: evac(q, (name, C * b + i, C * b + i + PIECE), bk, None, i) for i in range(0, C, PIECE)]
        early = {"V": pack + [lambda: tt(even(t1), odd(t0), JJ, A.not_equal), lambda: choose(t2, al("FAR"), t1), lambda: ts(tb(1), odd(t2), 0.5, None, A.mult)],
                 "S": [x for b in range(FEV, 3) for x in read("S", F, b, b)]}
        if r == 0:
            early["V"] = [lambda: tt(DL, odd(pairs), odd(t0), A.subtract), lambda: tt(odd(t1), DL, odd(pairs), A.add)] + early["V"]
        if r == 1:
            early["V"] += [lambda: quant("VQ", "VS", "VT")]

        def mp(q, x):
            return lambda: evac(q, (M, C * x[0] + x[1], C * x[0] + x[2]), 4 + x[0], None, x[1])
        late = {"V": [mp("V", x) for x in MV], "S": [mp("S", x) for x in MS]}

        def wait(k):
            for q in "VS":
                if len(late[q]) > NW - k + (q == "V"):
                    late[q].pop(0)()
                elif early[q]:
                    early[q].pop(0)()
        choose(t0, *sides[0])
        if r > 0:
            choose(t1, *sides[1])
        ts(tb(0), odd(t0), 0.5, None, A.mult)
        w = (WN, 0, C)
        both(w, IOS, tb(0), 10)
        cur, pt, pw = 0, 1, 1
        for k, step in enumerate(STEPS):
            wait(k)
            w2 = ("WK", 0, C) if k == len(STEPS) - 1 else (WN, C * k + C, C * k + 2 * C)
            if step == "g":
                both(w2, w, tb(cur), 10)
                w, pw = w2, pw + pt
            else:
                sc = ("SC", "SC3")[k % 2]
                scan(w, sc)
                both(w2, w, tb(cur), TGV[max(cur - 1, 0)])
                cur = max(cur + 1, 2)
                sample(tb(cur), sc)
                w, pt, pw = w2, pw, pw + pt
        assert 3 * pw >= C - 1 and not early["V"] and not early["S"]
        wait(NW - 2)
        scan(w)
        both(al("AW"), al("WK"), tb(1), TGV[-2])
        sample(tb(cur + 1))
        wait(NW - 1)
        scan(al("AW"), "SC3")
        both(("FW", 96, 96 + C), w, tb(cur + 1), TGV[-1])
        sample(tb(cur + 2), "SC3", 256.25)
        wait(NW)
        both(al(AS), al("FW"), tb(cur + 2), 10)
        late["V"].pop(0)()
        scan(al(AS))
        for x in MEND:
            mp("S", x)()
        assert not late["V"] and not late["S"]
        sample(al(AT))

        fi = part("FI", r + 1)
        if r == 0:
            def piece(q, lo, hi):
                gather(q, (Z, 64 * lo + 3, 64 * hi, 4), plane(M, 3), (AT, lo, hi))
            both(al("FS1"), al(FS), al(AT), 10)
            piece("V", 0, 4)
            for b in range(3):
                gather("S", lane(Z, b), plane(M, b), al(AT))
            scan(al("FS1"), "SC2")
            piece("V", 4, 8)
            sample(al("FT0"), "SC2")
            piece("V", 8, 12)
            piece("S", 12, 20)
            scatter(al("RI"), al("FT0"), 0, AHEAD)
        else:
            scatter(al("AI"), al(AT))
            for b in range(3):
                gather("S", lane(Z, b), plane(M, b), al(AT))
            both(lane(Z, 3), plane(M, 3), al(AT), ZV)
            gather("S", al("RI"), al("AI"), part("FI", r))
        for lo, hi in CUT:
            quant(QZ, SZ, Z, lo, hi)
        if r == 0:
            scatter(al("RI"), al("FT0"), AHEAD, 20)
        scan(al("RI"))
        if r == 0:
            ts(part("OL", 1), held("SC2"), K, 160.0, A.mult, A.add)
        sample(fi)
        if r == 0:
            offsets4(1, (3,))
        mm(0, "WQ", "WS", 0, QZ, SZ, c0=0, c1=H)
        mm(4, "WQ", "WS", 0, QZ, SZ, c0=H, c1=C)
        for b in (1, 3, 2):
            mm(4 + b, "WQ", "WS", 128 * b, QZ, SZ)
        evac("S", (PW, 0, H), 0, 0.015625)
        evac("S", (PW, H, C), 4, 0.015625)
        for b in (1, 3, 2):
            evac("S", plane(PW, b), 4 + b, 0.015625)
        gather("S", al(B3), plane(PW, 3), fi)
        if r == 1:
            gather("S", al("FS" + nxt), al(FS), al(AT))
        if r == 2:
            op("S", lambda: s.activation(T.LNF[:], T[FS][:].indirect(T[AT][:]), F_.Identity, bias=160.0), [reg(FS), reg(AT)], [reg("LNF")])
            dma("S", T.ln[:], T.LNF[0:128:16, :], [reg("LNF")], [], "out")
        for b in range(3):
            op("V", lambda: v.tensor_tensor(ap(lane("X" + nxt, b)), ap(plane(PW, b)).indirect(ap(fi)), ap(plane(F, b)), A.add),
               [rg(plane(PW, b)), rg(fi), rg(plane(F, b))], [rg(lane("X" + nxt, b))])
        for lo, hi in CUT:
            out = ("X" + nxt, 4 * lo + 3, 4 * hi, 4)
            op("V", lambda: v.tensor_tensor(ap(out), T[B3][:, lo:hi], ap(bank(3, lo, hi - lo)), A.add), [reg(B3), brg(3)], [rg(out)])
        for lo, hi in CUT:
            quant("QX" + nxt, "SX" + nxt, "X" + nxt, lo, hi)

    for i, (lo, hi) in enumerate(CUT):
        mm(4 + i, "VQ", "VS", 0, "QX3", "SX3", c0=lo, c1=hi)
    dma("Y", T.oc[:], u8(T.QX3[:]), [reg("QX3")], [], "out")
    evac("V", ("YS",) + CUT[0], 4)
    evac("S", ("YS",) + CUT[1], 5)
    dma("S", T.y[:], T.YS[:], [reg("YS")], [], "out")
    for k in range(4):
        dma("YYYS"[k], T.osc[4 * k:4 * k + 4, :], T.SX3[32 * k:32 * k + 4, :], [reg("SX3")], [], "out")
    for sem in sorted(count, key=lambda k: (k == "out", k in ("sP", "sV", "sS"))):
        g.wait_ge(T.sem[sem], count[sem])
